import numpy as np, ml_dtypes
CORES = [3,11,19,27,35,43]
N = 6
import mx_ref
BF = ml_dtypes.bfloat16
def entries(a):
    return np.ascontiguousarray(a.T).reshape(-1)
def table(e):
    return np.ascontiguousarray(np.reshape(e, (-1, 16)).T).astype(np.int32)
def f(rng, *shape):
    return mx_ref.flush((rng.standard_normal(shape, dtype=np.float32) * np.exp2(rng.integers(-2, 3, shape[:-1] + (1,)))).astype(BF))
def wide(rng, *shape, cols=0):
    v = rng.standard_normal(shape, dtype=np.float32) * np.exp2(rng.integers(-12, 13, shape)).astype(np.float32)
    if cols: v *= np.repeat(np.exp2(rng.integers(-cols, cols + 1, shape[:-2] + (1, shape[-1] // 4))) * (rng.random(shape[:-2] + (1, shape[-1] // 4)) > 0.0625), 4, axis=-1).astype(np.float32)
    return mx_ref.flush(v.astype(BF))
R, P, MOST = 5, 48, 5
def lists(rng, plan, tie=False):
    v = rng.integers(0, 1001, (N, R, P))
    hold = np.arange(P).reshape(N, 8)
    for t in range(R):
        for a in range(t % 2, N - 1, 2):
            A, B, go = v[a, t], v[a + 1, t], set(int(k) for k in plan(t, a))
            for k in range(8):
                p, q = int(hold[a, k]), int(hold[a + 1, k])
                if tie:
                    A[[p, q]] = rng.integers(300, 701, 2)
                    B[[p, q]] = A[[p, q]] + rng.integers(-200, 201)
                    if k in go: A[q] += 1
                else:
                    while A[q] + B[p] == A[p] + B[q]:
                        A[[p, q]] = rng.integers(0, 1001, 2)
                        B[[p, q]] = rng.integers(0, 1001, 2)
                    if (A[q] + B[p] > A[p] + B[q]) != (k in go):
                        A[[p, q]] = A[[q, p]]
                        B[[p, q]] = B[[q, p]]
                if k in go: hold[a, k], hold[a + 1, k] = q, p
    return {"dm": np.stack([table(e.reshape(-1)) for e in v])}
def setup_inputs(rng):
    return {"x": f(rng, N, 128, 512 * R), "w": f(rng, N, 128, 1024), **lists(rng, lambda t, a: rng.permutation(8)[:rng.integers(0, MOST + 1)])}
def setup_inputs_back(rng):
    go = rng.permutation(8)[:MOST]
    return {**setup_inputs(rng), **lists(rng, lambda t, a: [] if t % 2 else go)}
def setup_inputs_carry(rng):
    d = setup_inputs(rng)
    go = rng.permutation(8)[:MOST]
    c = rng.permutation(np.repeat([-5, 5], 4))
    e = np.where(np.arange(N)[:, None] % 2 == 0, c, -c)
    s = np.exp2(e).astype(np.float32)[:, None, :, None]
    d["w"] = mx_ref.flush((d["w"].astype(np.float32).reshape(N, 128, 8, 128) * s).reshape(N, 128, 1024).astype(BF))
    return {**d, **lists(rng, lambda t, a: go)}
def setup_inputs_equal(rng):
    return {**setup_inputs(rng), **lists(rng, lambda t, a: rng.permutation(8)[:MOST], tie=True)}
def setup_inputs_turn(rng):
    go = rng.permutation(8)
    return {**setup_inputs(rng), **lists(rng, lambda t, a: go[:MOST] if t < 2 else go[8 - MOST:])}
def setup_inputs_spread(rng):
    d = setup_inputs(rng); d["x"] = wide(rng, N, 128, 512 * R, cols=6); return d
def rounds(dm):
    v = np.stack([entries(e) for e in dm]).reshape(N, R, P)
    hold = np.arange(P).reshape(N, 8)
    held, most = [], 0
    for t in range(R):
        for a in range(t % 2, N - 1, 2):
            n = 0
            for k in range(8):
                p, q = int(hold[a, k]), int(hold[a + 1, k])
                if v[a, t, q] + v[a + 1, t, p] > v[a, t, p] + v[a + 1, t, q]:
                    hold[a, k], hold[a + 1, k] = q, p
                    n += 1
            most = max(most, n)
        held.append(np.array(hold))
    return held, most
def check_inputs(d):
    for n in ("x", "w"):
        m = np.abs(d[n].astype(np.float32))
        if not np.all((m == 0) | ((m >= 2.0 ** -30) & (m <= 2.0 ** 30))): return [n]
    if d["dm"].min() < 0 or d["dm"].max() > 1000: return ["dm"]
    return ["more than MOST slots change at a pair in a round"] if rounds(d["dm"])[1] > MOST else []
def reference(x, w, dm):
    held = rounds(dm)[0]
    y = np.zeros((N, 128, 256 * R), np.float32)
    for t in range(R):
        for r in range(N):
            X = mx_ref.quantize(np.ascontiguousarray(x[r][:, 512 * t:512 * t + 512]))
            for h in range(2):
                S = np.concatenate([w[p >> 3][:, 128 * (p & 7):128 * (p & 7) + 128] for p in held[t][r, 4 * h:4 * h + 4]], axis=1)
                y[r][:, 256 * t + 128 * h:256 * t + 128 * h + 128] = mx_ref.matmul(mx_ref.quantize(S), X)
    return {"y": y}

@@ -1,0 +1,482 @@
+from concourse.bass import DstId, RemoteDMATransfer
+from concourse.mybir import dt, AluOpType, ActivationFunctionType
+
+NR = 6
+RD = 5
+PC = 32
+LANES = 5
+BLK = LANES * PC
+OWN = 16 * PC
+W1 = OWN + 2 * BLK
+W3 = W1 + 2 * BLK
+LC = 9
+SB = 12 * PC - PC
+
+F32 = "float32"
+SCRATCH = {
+    "wt": ("sbuf", [128, 1024], "bfloat16"),
+    "xt": ("sbuf", [128, 512 * RD], "bfloat16"),
+    "lst": ("sbuf", [128, 56], "int32"),
+    "p1c": ("sbuf", [128, OWN], "float8_e4m3fn_x4"),
+    "p1s": ("sbuf", [128, OWN], "uint8"),
+    "p2c": ("sbuf", [128, W3], "float8_e4m3fn_x4"),
+    "p2s": ("sbuf", [128, W3], "uint8"),
+    "snd1c": ("sbuf", [128, SB], "float8_e4m3fn_x4"),
+    "snd1s": ("sbuf", [128, SB], "uint8"),
+    "snd3c": ("sbuf", [128, SB], "float8_e4m3fn_x4"),
+    "snd3s": ("sbuf", [128, SB], "uint8"),
+    "xq": ("sbuf", [128, 128 * RD], "float8_e4m3fn_x4"),
+    "xs": ("sbuf", [128, 128 * RD], "uint8"),
+    "yb": ("sbuf", [128, 256 * RD], F32),
+    "ps": ("psum", [128, 4096], F32),
+    "pi": ("sbuf", [128, 8], "int32"), "pf": ("sbuf", [128, 8], F32),
+    "z32": ("sbuf", [128, 32], F32), "k32": ("sbuf", [128, 64], F32), "kk": ("sbuf", [128, 64], F32),
+    "g40": ("sbuf", [128, 64], F32), "g96": ("sbuf", [128, 96], F32), "n96": ("sbuf", [128, 96], F32),
+    "base1": ("sbuf", [128, 64], F32), "base3": ("sbuf", [128, 64], F32),
+    "klist": ("sbuf", [128, 8], "uint16"), "rep": ("sbuf", [128, 12], "uint16"),
+    "gd": ("sbuf", [128, 64], F32), "xx": ("sbuf", [128, 96], F32), "kq": ("sbuf", [128, 272], F32),
+    "rec": ("sbuf", [128, 128], F32), "dk0": ("sbuf", [128, 4], F32), "d4": ("sbuf", [128, 4], F32),
+    "mk": ("sbuf", [128, 16], F32),
+    "dr0": ("sbuf", [128, 64], F32), "dr1": ("sbuf", [128, 64], F32), "dr2": ("sbuf", [128, 64], F32), "dr3": ("sbuf", [128, 64], F32),
+    "st0": ("sbuf", [128, 64], F32), "st1": ("sbuf", [128, 64], F32), "st2": ("sbuf", [128, 64], F32), "st3": ("sbuf", [128, 64], F32),
+    "me0": ("sbuf", [128, 32], F32), "me1": ("sbuf", [128, 64], F32), "me2": ("sbuf", [128, 96], F32), "me3": ("sbuf", [128, 64], F32), "me4": ("sbuf", [128, 32], F32),
+    "fm0": ("sbuf", [128, 32], F32), "fm1": ("sbuf", [128, 64], F32), "fm2": ("sbuf", [128, 96], F32), "fm3": ("sbuf", [128, 64], F32), "fm4": ("sbuf", [128, 32], F32),
+    "tm": ("sbuf", [128, 8], F32), "v0": ("sbuf", [128, 64], F32), "v1": ("sbuf", [128, 64], F32), "v2": ("sbuf", [128, 64], F32), "v3": ("sbuf", [128, 64], F32), "v4": ("sbuf", [128, 8], F32),
+    "in1": ("sbuf", [128, 64], F32), "ma1": ("sbuf", [128, 64], F32), "eq1": ("sbuf", [128, 96], F32), "pr1": ("sbuf", [128, 96], F32), "sc1": ("sbuf", [128, 96], F32),
+    "in3": ("sbuf", [128, 64], F32), "ma3": ("sbuf", [128, 64], F32), "eq3": ("sbuf", [128, 96], F32), "pr3": ("sbuf", [128, 96], F32), "sc3": ("sbuf", [128, 96], F32),
+    "bv": ("sbuf", [128, 64], F32), "q1": ("sbuf", [128, 64], F32), "q2": ("sbuf", [128, 64], F32), "q3": ("sbuf", [128, 64], F32),
+    "e2": ("sbuf", [128, 8], F32), "f2": ("sbuf", [128, 8], F32), "out3": ("sbuf", [128, 64], F32),
+    "r1": ("sbuf", [128, 64], F32), "ret": ("sbuf", [128, 64], F32), "far": ("sbuf", [128, 8], F32), "bf": ("sbuf", [128, 64], F32),
+    "nret": ("sbuf", [128, 64], F32), "nr32": ("sbuf", [128, 64], F32), "w1": ("sbuf", [128, 64], F32), "w2": ("sbuf", [128, 64], F32), "w3": ("sbuf", [128, 64], F32), "w4": ("sbuf", [128, 64], F32),
+    "a1": ("sbuf", [128, 64], F32), "a2": ("sbuf", [128, 64], F32), "a3": ("sbuf", [128, 64], F32),
+    "e4": ("sbuf", [128, 8], F32), "f4": ("sbuf", [128, 8], F32),
+    "off1": ("sbuf", [128, 24], "uint16"), "off3": ("sbuf", [128, 24], "uint16"),
+}
+for _t in range(RD):
+    SCRATCH["offs%d" % _t] = ("sbuf", [128, 16], "uint16")
+    SCRATCH["sc%d" % _t if _t not in (1, 3) else "sk%d" % _t] = ("sbuf", [128, 256], "float8_e4m3fn_x4")
+    SCRATCH["ss%d" % _t] = ("sbuf", [128, 256], "uint8")
+SC_NAME = ["sc0", "sk1", "sc2", "sk3", "sc4"]
+
+SEMAPHORES = ["v", "a", "mm", "gi", "sdm", "sw", "sx", "scp", "sy", "al", "aw", "ar1", "ar3", "loc"]
+
+ADD, SUB, MUL, MIN = AluOpType.add, AluOpType.subtract, AluOpType.mult, AluOpType.min
+LT, GT, EQ = AluOpType.is_lt, AluOpType.is_gt, AluOpType.is_equal
+AND, SHR = AluOpType.bitwise_and, AluOpType.logical_shift_right
+COPY = ActivationFunctionType.Copy
+
+
+def rank_program(g, core, T, topo):
+    r = T.rank_of(core)
+    if r is None:
+        return
+    cores = T.cores
+    pair = r // 2
+    base, e = 2 * pair, r % 2
+    mid = pair == 1
+    vec = g.vector
+    S = T.sem
+
+    near = None if mid else (0 if pair == 0 else 1)
+    NB = slice(0, 40) if mid else slice(32 * near, 32 * near + 8)
+    low = 0 if mid else 1
+    mine = low if e == 0 else 1 - low
+    far = None if mid else 1 - near
+
+    def blk(name, b):
+        return T[name][:, 32 * b:32 * b + 8]
+
+    def sender(s, q):
+        for m in (2 * s, 2 * s + 1):
+            if topo.same_plane(topo.chip(cores[m]), topo.chip(cores[q])):
+                return m
+        return 2 * s
+
+    def peers(s):
+        return [q for q in (2 * s, 2 * s + 1) if sender(pair, q) == r]
+
+    n_off = len(topo.engines(core, cores[base + 1 - e]))
+
+    def addr(q):
+        rid, pid, _ = topo.addr(cores[q])
+        return rid, pid
+
+    st = {"v": 0, "vw": 0, "a": 0, "aw": 0, "loc": 0}
+
+    def V(call, args, deps=()):
+        need = max([0] + list(deps))
+        if need > st["vw"]:
+            vec.wait_ge(S.v, need)
+            st["vw"] = need
+        call(*args).then_inc(S.v, 1)
+        st["v"] += 1
+        return st["v"]
+
+    def ts(out, in0, s1, op0, deps=(), s2=None, op1=None):
+        if op1 is None:
+            return V(vec.tensor_scalar, (out, in0, s1, None, op0), deps)
+        return V(vec.tensor_scalar, (out, in0, s1, s2, op0, op1), deps)
+
+    def tt(out, a, b, op, deps=()):
+        return V(vec.tensor_tensor, (out, a, b, op), deps)
+
+    def tr(out, a, deps=()):
+        return V(vec.transpose, (out, a), deps)
+
+    def scan(out, d0, d1, deps=()):
+        return V(vec.tensor_tensor_scan, (out, d0, d1, 0.0, MUL, ADD), deps)
+
+    mycol = T.lst[:, LC * r:LC * r + LC]
+    for b in range(4):
+        for h, q in ((0, g.sync), (1, g.scalar)):
+            p0 = 32 * b + 16 * h
+            q.dma_start(T.lst[p0:p0 + 16, LC * r:LC * r + LC], T.dm[:, 6 * h:6 * h + LC]).then_inc(S.sdm, 16)
+    g.sync.dma_start(T.wt[:], T.w[:]).then_inc(S.sw, 16)
+
+    g.iota(T.pi[:, 0:1], [[0, 1]], 0, 1).then_inc(S.gi, 1)
+    g.iota(T.k32[:], [[0, 2], [32, 32]], 0, 0, allow_small_or_imprecise_dtypes=True).then_inc(S.gi, 1)
+    g.iota(T.kk[:], [[0, 2], [1, 32]], 0, 0, allow_small_or_imprecise_dtypes=True).then_inc(S.gi, 1)
+    g.iota(T.pr1[:], [[0, 12], [1, 8]], 0, 0, allow_small_or_imprecise_dtypes=True).then_inc(S.gi, 1)
+    g.iota(T.n96[:], [[0, 2], [1, 6], [0, 8]], 1, 0, allow_small_or_imprecise_dtypes=True).then_inc(S.gi, 1)
+
+    def fill(name, val, cols=None):
+        ap = T[name][:] if cols is None else T[name][:, cols]
+        return V(vec.memset, (ap, val))
+    fill("z32", 0.0)
+    fill("gd", 0.0)
+    fill("xx", 0.0)
+    fill("kq", 0.0, slice(256, 272))
+    for n in ("st0", "st1", "st2", "st3", "v0", "out3"):
+        fill(n, 0.0)
+    if not mid:
+        fill("me2", 0.0)
+    fill("base1", float(OWN - PC), slice(0, 32))
+    fill("base1", float(OWN + BLK - PC), slice(32, 64))
+    fill("base3", float(W1 - PC), slice(0, 32))
+    tf = fill("base3", float(W1 + (BLK if mid else 0) - PC), slice(32, 64))
+    vec.wait_ge(S.gi, 5)
+    P = T.pi
+    c15 = ts(P[:, 1:2], P[:, 0:1], 15, AND)
+    c7 = ts(P[:, 2:3], P[:, 0:1], 7, AND)
+    c3 = ts(P[:, 3:4], P[:, 0:1], 3, AND)
+    ch = ts(P[:, 4:5], P[:, 0:1], 2, SHR, (), 3, AND)
+    ts(T.g40[:], T.kk[:], 1.0, MIN)
+    tg = ts(T.g96[:], T.pr1[:], 1.0, MIN)
+    F = T.pf
+    f15 = V(vec.tensor_copy, (F[:, 0:1], P[:, 1:2]), (c15,))
+    f7 = V(vec.tensor_copy, (F[:, 2:3], P[:, 2:3]), (c7,))
+    f3 = V(vec.tensor_copy, (F[:, 3:4], P[:, 3:4]), (c3,))
+    fh = ts(F[:, 4:5], P[:, 4:5], 18.0, MUL, (ch,))
+    ts(F[:, 1:2], F[:, 0:1], 16.0, ADD, (f15,))
+    ts(T.kk[:], T.k32[:], 256.0, ADD, (tg,))
+    fv = tt(F[:, 5:6], F[:, 4:5], F[:, 3:4], ADD, (fh, f3))
+    ts(T.rep[:, 0:3], T.z32[:, 0:3], F[:, 2:3], ADD, (f7,))
+    ts(T.rep[:, 3:9], T.z32[:, 0:6], F[:, 2:3], ADD, (f7,), 32.0, ADD)
+    for o in range(2):
+        for t in range(1, RD):
+            half, t1 = (0, t) if t <= 2 else (1, t - 2)
+            tc = ts(T.klist[:, 4 * o + t - 1:4 * o + t], F[:, 5:6], float(64 * (2 * half + o) + LC * (t % 2) + 3 * t1), ADD, (fv,))
+
+    g.wait_ge(S.sdm, 128)
+    others = [q for q in range(NR) if q != r]
+    g.remote_dma_fused([RemoteDMATransfer(
+        dst_ids=[DstId(rid=addr(q)[0], pnc=addr(q)[1]) for q in others], dma_engine_mask=topo.mask(core, cores[others[0]]),
+        remote_sem=S.al, srcs=[mycol], dsts=[mycol] * len(others))], local_sem=S.loc)
+    st["loc"] += n_off
+
+    vec.wait_ge(S.sw, 16)
+    my = slice(8 * PC * e, 8 * PC * (e + 1))
+    tw = V(vec.quantize_mx, (T.p1c[:, my], T.p1s[:, my], T.wt[:]))
+    g.wait_ge(S.v, tw)
+    mate = base + 1 - e
+    rid, pid = addr(mate)
+    mk = topo.mask(core, cores[mate])
+    g.remote_dma(T.p1c[:, my].bitcast(dt.uint8), T.p1c[:, my].bitcast(dt.uint8), S.aw, S.loc, pid, rid, mk)
+    g.remote_dma(T.p1s[:, my], T.p1s[:, my], S.aw, S.loc, pid, rid, mk)
+    st["loc"] += 2 * n_off
+    g.sync.wait_ge(S.v, tw)
+    g.sync.dma_start(T.xt[:], T.x[:]).then_inc(S.sx, 16)
+
+    vec.wait_ge(S.sdm, 128)
+    vec.wait_ge(S.al, (NR - 1) * n_off)
+    k = tt(T.gd[:, 0:5 * LC], T.lst[:, 0:5 * LC], T.lst[:, LC:6 * LC], SUB, (tf,))
+    k = tr(T.xx[:, 0:64], T.gd[:], (k,))
+    for q in range(4):
+        kq = tr(T.kq[:, 64 * q:64 * q + 64], T.xx[:, 8 * q:8 * q + 64], (k,))
+    E0, O0 = 0, 64
+    E = lambda a, b: T.rec[:, E0 + a:E0 + b]
+    O = lambda a, b: T.rec[:, O0 + a:O0 + b]
+
+    def widen(me, b, key, deps):
+        return ts(T[me][:, 32 * b:32 * b + 32], T.z32[:], key, LT, deps)
+
+    d = tt(T.dk0[:, 0:3], T.kq[:, 64:103:19], T.kq[:, 0:39:19], SUB, (kq,))
+    kr = V(vec.tensor_copy, (T.rec[:], T.kq[:].indirect(T.klist[:])), (kq, tc))
+    m = ts(T.mk[:, 0:3], T.dk0[:, 0:3], 0.0, GT, (d,))
+    w0 = widen("me0", 0, T.dk0[:, pair:pair + 1], (d,))
+    d = tt(T.dr0[:], O(0, 64), E(0, 64), SUB, (kr,))
+    x0 = tr(T.fm0[:], T.me0[:], (w0,))
+    for c in range(3):
+        s = ts(T.st0[:, c:64:4], T.dr0[:, c:64:4], T.mk[:, c:c + 1], MUL, (d, m))
+    u1 = tt(E(0, 64), E(0, 64), T.st0[:], ADD, (s,))
+    u2 = tt(O(0, 64), O(0, 64), T.st0[:], SUB, (s,))
+    t1 = ts(T.tm[:], T.fm0[:, 0:8], 256.0, MUL, (x0,))
+    d1 = tt(T.dr1[:, 0:63], E(1, 64), O(0, 63), SUB, (u2,))
+    vl = tt(blk("v0", low), T.tm[:], T.k32[:, 0:8], ADD, (t1,))
+    w1 = [widen("me1", b, T.dr1[:, 5 * b:5 * b + 1], (d1,)) for b in range(2)]
+    v0 = tt(blk("v0", 1 - low), T.kk[:, 0:8], T.tm[:], SUB, (t1,))
+    x1 = tr(T.fm1[:], T.me1[:], (w1[1],))
+    m1 = ts(T.mk[:, 4:6], T.dr1[:, 0:6:5], 0.0, GT, (d1,))
+
+    def lanes(i, fm, src, blocks, fillers):
+        inc, ma, eq, pr, sc, off = ["%s%d" % (n, i) for n in ("in", "ma", "eq", "pr", "sc", "off")]
+        if i == 1:
+            sc = "sc1"
+        nn = 48 * len(blocks)
+        rc = (0, 6) if len(blocks) == 2 else ((0, 3) if blocks[0] == 0 else (6, 9))
+        rep = T.rep[:, rc[0]:rc[1]]
+        fillers = list(fillers)
+
+        def fl():
+            if fillers:
+                fillers.pop(0)()
+        ti = scan(T[inc][:, 0:40], T.g40[:, 0:40], T[fm][:, 0:40], (x1 if i == 1 else x3[0],))
+        tm = tt(T[ma][:, 0:40], T[fm][:, 0:40], T[src][:, 0:40], MUL, (v0 if i == 1 else x3[1],))
+        q = tt(T[eq][:, 0:nn], T[inc][:, 0:40].indirect(rep), T.n96[:, 0:nn], EQ, (ti,))
+        fl()
+        q = tt(T[pr][:, 0:nn], T[ma][:, 0:40].indirect(rep), T[eq][:, 0:nn], MUL, (q, tm))
+        fl()
+        q = scan(T[sc][:, 0:nn], T.g96[:, 0:nn], T[pr][:, 0:nn], (q,))
+        fl()
+        fl()
+        cols = 12 * len(blocks)
+        ts(T[off][:, 0:cols:2], T[sc][:, 7:nn:8], F[:, 0:1], ADD, (q,))
+        q = ts(T[off][:, 1:cols:2], T[sc][:, 7:nn:8], F[:, 1:2], ADD, (q,))
+        return ti, q
+
+    def pick(dst_c, dst_s, src_c, src_s, width, off, n, deps, waits):
+        for sem, val in waits:
+            vec.wait_ge(sem, val)
+            g.scalar.wait_ge(sem, val)
+        q = V(vec.tensor_copy, (T[dst_c][:, 0:16 * n].bitcast(dt.uint32), T[src_c][:, 0:width].bitcast(dt.uint32).indirect(T[off][:, 0:n])), deps)
+        g.scalar.wait_ge(S.v, max(deps))
+        g.scalar.activation(T[dst_s][:, 0:16 * n], T[src_s][:, 0:width].indirect(T[off][:, 0:n]), COPY).then_inc(S.a, 1)
+        st["a"] += 1
+        return q, st["a"]
+
+    def send(i, jobs, pk):
+        sem = S["ar%d" % i]
+        g.wait_ge(S.v, pk[0])
+        eng = topo.engines(core, cores[jobs[0][1]])
+        per = len(eng) // len(jobs)
+        for kind in ("c", "s"):
+            if kind == "s":
+                g.wait_ge(S.a, pk[1])
+            sb, pb = T["snd%d%s" % (i, kind)], T["p2%s" % kind]
+            trs = []
+            for n, (a, q, p) in enumerate(jobs):
+                mask = sum(1 << x for x in eng[per * n:per * n + per])
+                src, dst = sb[:, a:a + BLK], pb[:, p:p + BLK]
+                if kind == "c":
+                    src, dst = src.bitcast(dt.uint8), dst.bitcast(dt.uint8)
+                trs.append(RemoteDMATransfer(dst_ids=[DstId(rid=addr(q)[0], pnc=addr(q)[1])], dma_engine_mask=mask,
+                                             remote_sem=sem, srcs=[src], dsts=[dst]))
+            g.remote_dma_fused(trs, local_sem=S.loc)
+            st["loc"] += per * len(jobs)
+
+    hold = {}
+
+    def f_step1a():
+        hold["a"] = ts(T.st1[:, 16:63:4], T.dr1[:, 16:63:4], T.mk[:, 4:5], MUL, (m1,))
+
+    def f_step1b():
+        hold["b"] = ts(T.st1[:, 17:63:4], T.dr1[:, 17:63:4], T.mk[:, 5:6], MUL, (m1,))
+
+    def f_o1():
+        hold["o"] = tt(O(16, 63), O(16, 63), T.st1[:, 16:63], ADD, (hold["b"],))
+
+    def f_e1():
+        hold["e"] = tt(E(17, 64), E(17, 64), T.st1[:, 16:63], SUB, (hold["b"],))
+
+    near_blocks = [0, 1] if mid else [near]
+    ti1, to1 = lanes(1, "fm1", "v0", near_blocks, [f_step1a, f_step1b, f_o1, f_e1])
+    GA = 6 * PC
+    pk1 = pick("snd1c", "snd1s", "p1c", "p1s", OWN, "off1", 22 if mid else 10, (to1,), [(S.aw, 2 * n_off)])
+    jobs = []
+    for n, b in enumerate(near_blocks):
+        s = pair - 1 if b == pair - 1 else pair + 1
+        for q in peers(s):
+            jobs.append((GA * n, q, OWN + BLK * b))
+    send(1, jobs, pk1)
+    g.sync.wait_ge(S.aw, 2 * n_off)
+    g.sync.wait_ge(S.v, pk1[0])
+    g.sync.dma_start(T.p2c[:, 0:OWN].bitcast(dt.uint8), T.p1c[:, 0:OWN].bitcast(dt.uint8)).then_inc(S.scp, 16)
+    g.sync.dma_start(T.p2s[:, 0:OWN], T.p1s[:, 0:OWN]).then_inc(S.scp, 16)
+
+    d2 = tt(T.dr2[:, 16:64], O(16, 64), E(16, 64), SUB, (hold["e"],))
+    tq = ts(T.q1[:, NB], T.in1[:, NB], 32.0, MUL, (ti1,))
+    tb = tt(T.bv[:, NB], T.base1[:, NB], T.v0[:, NB], SUB, (v0,))
+    m2 = ts(T.mk[:, 8:11], T.dr2[:, 16:27:5], 0.0, GT, (d2,))
+    order = [(0, 0), (1, 2), (2, 1)] if mid else [(near, 1), (2, pair)]
+    for b, c in order:
+        w2 = widen("me2", b, T.dr2[:, 16 + 5 * c:17 + 5 * c], (d2,))
+    tq = tt(T.q2[:, NB], T.q1[:, NB], T.bv[:, NB], ADD, (tq, tb))
+    x2 = tr(T.fm2[:], T.me2[:], (w2,))
+    for c in range(3):
+        s = ts(T.st2[:, 32 + c:64:4], T.dr2[:, 32 + c:64:4], T.mk[:, 8 + c:9 + c], MUL, (m2,))
+    tq = tt(T.q3[:, NB], T.fm1[:, NB], T.q2[:, NB], MUL, (tq,))
+    u1 = tt(E(32, 64), E(32, 64), T.st2[:, 32:64], ADD, (s,))
+    u2 = tt(O(32, 64), O(32, 64), T.st2[:, 32:64], SUB, (s,))
+    tv1 = tt(T.v1[:, NB], T.v0[:, NB], T.q3[:, NB], ADD, (tq,))
+    d3 = tt(T.dr3[:, 32:63], E(33, 64), O(32, 63), SUB, (u2,))
+    V1 = [blk("v1" if mid or b == near else "v0", b) for b in range(2)]
+    td = tt(T.e2[:], V1[1], V1[0], SUB, (tv1,))
+    for b in range(2):
+        w3 = widen("me3", b, T.dr3[:, 32 + 5 * b:33 + 5 * b], (d3,))
+    td = tt(T.f2[:], T.fm2[:, 64:72], T.e2[:], MUL, (td, x2))
+    x3t = tr(T.fm3[:], T.me3[:], (w3,))
+    m3 = ts(T.mk[:, 12:14], T.dr3[:, 32:38:5], 0.0, GT, (d3,))
+    ta = tt(blk("v2", 0), V1[0], T.f2[:], ADD, (td,))
+    tv2 = tt(blk("v2", 1), V1[1], T.f2[:], SUB, (td,))
+    if mid:
+        ts(T.out3[:, 0:8], T.v2[:, 0:8], float(OWN - PC), MIN, (ta,))
+        to3 = ts(T.out3[:, 32:40], T.v2[:, 32:40], float(OWN - PC), MIN, (tv2,))
+    else:
+        V(vec.tensor_copy, (blk("out3", far), blk("v0", near)))
+        to3 = ts(blk("out3", near), blk("v2", near), float(OWN - PC), MIN, (tv2,))
+    x3 = (x3t, max(to3, x3t))
+    ti3, tf3 = lanes(3, "fm3", "out3", [0, 1], [])
+    pk3 = pick("snd3c", "snd3s", "p1c", "p1s", OWN, "off3", 22, (tf3,), [])
+    jobs = []
+    for b in range(2):
+        if mid:
+            dst, col = 2 * b, W1
+        elif b == near:
+            dst, col = 1, W1 + (BLK if pair == 2 else 0)
+        else:
+            dst, col = 2 - pair, W1 + BLK
+        for q in peers(dst):
+            jobs.append((GA * b, q, col))
+    send(3, jobs, pk3)
+
+    def offs(t, v, deps):
+        ts(T["offs%d" % t][:, 0:16:2], v, F[:, 0:1], ADD, deps)
+        return ts(T["offs%d" % t][:, 1:16:2], v, F[:, 1:2], ADD, deps)
+
+    def tile(t, src, width, dep, waits):
+        return pick(SC_NAME[t], "ss%d" % t, src + "c", src + "s", width, "offs%d" % t, 16, (dep,), waits)
+
+    def products(t, pk, first):
+        g.tensor.wait_ge(S.v, max(pk[0], first))
+        g.tensor.wait_ge(S.a, pk[1])
+        for h in range(2):
+            bank = 512 * ((2 * t + h) % 8)
+            g.tensor.matmul_mx(T.ps[:, bank:bank + 128], T[SC_NAME[t]][:, 128 * h:128 * h + 128], T["ss%d" % t][:, 128 * h:128 * h + 128],
+                               T.xq[:, 128 * t:128 * t + 128], T.xs[:, 128 * t:128 * t + 128], True, True).then_inc(S.mm, 1)
+
+    def out_of(t, h):
+        bank = 512 * ((2 * t + h) % 8)
+        c = 256 * t + 128 * h
+        return T.yb[:, c:c + 128], T.ps[:, bank:bank + 128]
+
+    def evac_s(t, h):
+        o, i = out_of(t, h)
+        g.scalar.wait_ge(S.mm, 2 * t + h + 1)
+        g.scalar.activation(o, i, COPY).then_inc(S.a, 1)
+        st["a"] += 1
+
+    def evac_v(t, h):
+        o, i = out_of(t, h)
+        vec.wait_ge(S.mm, 2 * t + h + 1)
+        return V(vec.tensor_copy, (o, i))
+
+    def store(t, va, aa):
+        if va:
+            g.sync.wait_ge(S.v, va)
+        g.sync.wait_ge(S.a, aa)
+        g.sync.dma_start(T.y[:, 256 * t:256 * t + 256], T.yb[:, 256 * t:256 * t + 256]).then_inc(S.sy, 16)
+
+    vec.wait_ge(S.sx, 16)
+    xqt = []
+    for t in range(RD):
+        xqt.append(V(vec.quantize_mx, (T.xq[:, 128 * t:128 * t + 128], T.xs[:, 128 * t:128 * t + 128], T.xt[:, 512 * t:512 * t + 512])))
+        if t == 0:
+            q = offs(0, blk("v0", mine), (v0,))
+            pk = tile(0, "p1", OWN, q, [])
+            products(0, pk, xqt[0])
+    for h in range(2):
+        evac_s(0, h)
+    store(0, 0, st["a"])
+
+    n_in1 = 0
+    for s in ([0, 2] if mid else [1]):
+        n_in1 += 2 * (n_off // 2 if s == 1 else n_off)
+    q1 = offs(1, V1[mine], (tv1,))
+    q2 = offs(2, blk("v2", mine), (ta, tv2))
+    pk = tile(1, "p2", W1, q1, [(S.scp, 32), (S.ar1, n_in1)])
+    products(1, pk, xqt[1])
+    pk = tile(2, "p2", W1, q2, [])
+    products(2, pk, xqt[2])
+    for t in (1, 2):
+        for h in range(2):
+            evac_s(t, h)
+        store(t, 0, st["a"])
+
+    a = tt(T.r1[:, NB], T.fm1[:, NB], T.fm2[:, NB], MUL, (x2,))
+    if not mid:
+        fa = tt(T.far[:], blk("fm1", far), blk("fm2", near), MUL, (x2,))
+    s = ts(T.st3[:, 48:63:4], T.dr3[:, 48:63:4], T.mk[:, 12:13], MUL, (m3,))
+    s = ts(T.st3[:, 49:63:4], T.dr3[:, 49:63:4], T.mk[:, 13:14], MUL, (m3,))
+    rt = tt(T.ret[:, NB], T.fm1[:, NB], T.r1[:, NB], SUB, (a,))
+    if mid:
+        bf = T.base3[:, NB]
+        tbf = 0
+    else:
+        tbf = ts(blk("bf", near), T.far[:], float(BLK), MUL, (fa,), float(W1 - PC), ADD)
+        bf = T.bf[:, NB]
+    uo = tt(O(48, 63), O(48, 63), T.st3[:, 48:63], ADD, (s,))
+    ue = tt(E(49, 64), E(49, 64), T.st3[:, 48:63], SUB, (s,))
+    nt = ts(T.nret[:, NB], T.ret[:, NB], -1.0, MUL, (rt,), 1.0, ADD)
+    n3 = ts(T.nr32[:, NB], T.ret[:, NB], -32.0, MUL, (rt,), 32.0, ADD)
+    wb = tt(T.w2[:, NB], T.ret[:, NB], T.v0[:, NB], MUL, (rt,))
+    kc = 48 + 5 * pair
+    d4 = tt(T.d4[:, 0:1], O(kc, kc + 1), E(kc, kc + 1), SUB, (ue,))
+    wa = tt(T.w1[:, NB], T.nret[:, NB], bf, MUL, (nt, tbf))
+    a1 = tt(T.a1[:, NB], T.nr32[:, NB], T.in3[:, NB], MUL, (n3, ti3))
+    w4 = widen("me4", 0, T.d4[:, 0:1], (d4,))
+    wc = tt(T.w3[:, NB], T.w1[:, NB], T.w2[:, NB], ADD, (wa, wb))
+    x4 = tr(T.fm4[:], T.me4[:], (w4,))
+    if mid:
+        tt(blk("w4", 0), blk("w3", 0), blk("v2", 0), SUB, (wc,))
+        wd = tt(blk("w4", 1), blk("w3", 1), blk("v2", 1), SUB, (wc,))
+        parts = [0, 1]
+    else:
+        wd = tt(blk("w4", near), blk("w3", near), blk("v2", near), SUB, (wc,))
+        parts = [near]
+    for b in parts:
+        a2 = tt(blk("a2", b), blk("a1", b), blk("w4", b), ADD, (a1, wd))
+    for b in parts:
+        a3 = tt(blk("a3", b), blk("fm3", b), blk("a2", b), MUL, (a2,))
+    for b in parts:
+        tv3 = tt(blk("v3", b), blk("v2", b), blk("a3", b), ADD, (a3,))
+    V3 = [blk("v3" if mid or b == near else "v2", b) for b in range(2)]
+    q3 = offs(3, V3[mine], (tv3,))
+    td = tt(T.e4[:], V3[1], V3[0], SUB, (tv3,))
+    td = tt(T.f4[:], T.fm4[:, 0:8], T.e4[:], MUL, (td, x4))
+    td = tt(T.v4[:], V3[mine], T.f4[:], ADD if mine == 0 else SUB, (td,))
+    q4 = offs(4, T.v4[:], (td,))
+
+    n_in3 = 2 * 2 * (n_off // 2)
+    pk = tile(3, "p2", W3, q3, [(S.ar3, n_in3)])
+    products(3, pk, xqt[3])
+    pk = tile(4, "p2", W3, q4, [])
+    g.tensor.wait_ge(S.a, 9)
+    products(4, pk, xqt[4])
+    va = evac_v(3, 0)
+    evac_s(3, 1)
+    store(3, va, st["a"])
+    va = evac_v(4, 0)
+    evac_s(4, 1)
+    store(4, va, st["a"])
+    g.sync.wait_ge(S.sy, 16 * RD)
+    g.wait_ge(S.loc, st["loc"])

@@ -11,59 +11,54 @@ W1 = OWN + 2 * BLK
 W3 = W1 + 2 * BLK
 LC = 9
 SB = 12 * PC - PC
+XA = 3
 
 F32 = "float32"
 SCRATCH = {
     "wt": ("sbuf", [128, 1024], "bfloat16"),
     "xt": ("sbuf", [128, 512 * RD], "bfloat16"),
     "lst": ("sbuf", [128, 56], "int32"),
-    "p1c": ("sbuf", [128, OWN], "float8_e4m3fn_x4"),
-    "p1s": ("sbuf", [128, OWN], "uint8"),
-    "p2c": ("sbuf", [128, W3], "float8_e4m3fn_x4"),
-    "p2s": ("sbuf", [128, W3], "uint8"),
-    "snd1c": ("sbuf", [128, SB], "float8_e4m3fn_x4"),
-    "snd1s": ("sbuf", [128, SB], "uint8"),
-    "snd3c": ("sbuf", [128, SB], "float8_e4m3fn_x4"),
-    "snd3s": ("sbuf", [128, SB], "uint8"),
-    "xq": ("sbuf", [128, 128 * RD], "float8_e4m3fn_x4"),
-    "xs": ("sbuf", [128, 128 * RD], "uint8"),
+    "p1c": ("sbuf", [128, OWN], "float8_e4m3fn_x4"), "p1s": ("sbuf", [128, OWN], "uint8"),
+    "p2c": ("sbuf", [128, W3], "float8_e4m3fn_x4"), "p2s": ("sbuf", [128, W3], "uint8"),
+    "snd1c": ("sbuf", [128, SB], "float8_e4m3fn_x4"), "snd1s": ("sbuf", [128, SB], "uint8"),
+    "snd3c": ("sbuf", [128, SB], "float8_e4m3fn_x4"), "snd3s": ("sbuf", [128, SB], "uint8"),
+    "xqc": ("sbuf", [128, 128 * RD], "float8_e4m3fn_x4"), "xqs": ("sbuf", [128, 128 * RD], "uint8"),
     "yb": ("sbuf", [128, 256 * RD], F32),
     "ps": ("psum", [128, 4096], F32),
-    "pi": ("sbuf", [128, 8], "int32"), "pf": ("sbuf", [128, 8], F32),
-    "z32": ("sbuf", [128, 32], F32), "k32": ("sbuf", [128, 64], F32), "kk": ("sbuf", [128, 64], F32),
-    "g40": ("sbuf", [128, 64], F32), "g96": ("sbuf", [128, 96], F32), "n96": ("sbuf", [128, 96], F32),
-    "base1": ("sbuf", [128, 64], F32), "base3": ("sbuf", [128, 64], F32),
+    "pi": ("sbuf", [128, 8], "int32"),
     "klist": ("sbuf", [128, 8], "uint16"), "rep": ("sbuf", [128, 12], "uint16"),
-    "gd": ("sbuf", [128, 64], F32), "xx": ("sbuf", [128, 96], F32), "kq": ("sbuf", [128, 272], F32),
-    "rec": ("sbuf", [128, 128], F32), "dk0": ("sbuf", [128, 4], F32), "d4": ("sbuf", [128, 4], F32),
-    "mk": ("sbuf", [128, 16], F32),
-    "dr0": ("sbuf", [128, 64], F32), "dr1": ("sbuf", [128, 64], F32), "dr2": ("sbuf", [128, 64], F32), "dr3": ("sbuf", [128, 64], F32),
-    "st0": ("sbuf", [128, 64], F32), "st1": ("sbuf", [128, 64], F32), "st2": ("sbuf", [128, 64], F32), "st3": ("sbuf", [128, 64], F32),
-    "me0": ("sbuf", [128, 32], F32), "me1": ("sbuf", [128, 64], F32), "me2": ("sbuf", [128, 96], F32), "me3": ("sbuf", [128, 64], F32), "me4": ("sbuf", [128, 32], F32),
-    "fm0": ("sbuf", [128, 32], F32), "fm1": ("sbuf", [128, 64], F32), "fm2": ("sbuf", [128, 96], F32), "fm3": ("sbuf", [128, 64], F32), "fm4": ("sbuf", [128, 32], F32),
-    "tm": ("sbuf", [128, 8], F32), "v0": ("sbuf", [128, 64], F32), "v1": ("sbuf", [128, 64], F32), "v2": ("sbuf", [128, 64], F32), "v3": ("sbuf", [128, 64], F32), "v4": ("sbuf", [128, 8], F32),
-    "in1": ("sbuf", [128, 64], F32), "ma1": ("sbuf", [128, 64], F32), "eq1": ("sbuf", [128, 96], F32), "pr1": ("sbuf", [128, 96], F32), "sc1": ("sbuf", [128, 96], F32),
-    "in3": ("sbuf", [128, 64], F32), "ma3": ("sbuf", [128, 64], F32), "eq3": ("sbuf", [128, 96], F32), "pr3": ("sbuf", [128, 96], F32), "sc3": ("sbuf", [128, 96], F32),
-    "bv": ("sbuf", [128, 64], F32), "q1": ("sbuf", [128, 64], F32), "q2": ("sbuf", [128, 64], F32), "q3": ("sbuf", [128, 64], F32),
-    "e2": ("sbuf", [128, 8], F32), "f2": ("sbuf", [128, 8], F32), "out3": ("sbuf", [128, 64], F32),
-    "r1": ("sbuf", [128, 64], F32), "ret": ("sbuf", [128, 64], F32), "far": ("sbuf", [128, 8], F32), "bf": ("sbuf", [128, 64], F32),
-    "nret": ("sbuf", [128, 64], F32), "nr32": ("sbuf", [128, 64], F32), "w1": ("sbuf", [128, 64], F32), "w2": ("sbuf", [128, 64], F32), "w3": ("sbuf", [128, 64], F32), "w4": ("sbuf", [128, 64], F32),
-    "a1": ("sbuf", [128, 64], F32), "a2": ("sbuf", [128, 64], F32), "a3": ("sbuf", [128, 64], F32),
-    "e4": ("sbuf", [128, 8], F32), "f4": ("sbuf", [128, 8], F32),
     "off1": ("sbuf", [128, 24], "uint16"), "off3": ("sbuf", [128, 24], "uint16"),
 }
 for _t in range(RD):
-    SCRATCH["offs%d" % _t] = ("sbuf", [128, 16], "uint16")
-    SCRATCH["sc%d" % _t if _t not in (1, 3) else "sk%d" % _t] = ("sbuf", [128, 256], "float8_e4m3fn_x4")
-    SCRATCH["ss%d" % _t] = ("sbuf", [128, 256], "uint8")
-SC_NAME = ["sc0", "sk1", "sc2", "sk3", "sc4"]
+    SCRATCH["of%d" % _t] = ("sbuf", [128, 16], "uint16")
+    SCRATCH["st%dc" % _t] = ("sbuf", [128, 256], "float8_e4m3fn_x4")
+    SCRATCH["st%ds" % _t] = ("sbuf", [128, 256], "uint8")
+_WORK = {
+    "pf": 8, "z32": 32, "k32p": 32, "mod32": 64, "g40": 64, "mod8": 96, "g96": 96, "n96": 96, "base1": 64, "base3": 64,
+    "gd": 64, "xx": 96, "kq": 272, "rec": 128, "dk0": 4, "d4": 4, "mk": 16, "m256": 4,
+    "dr0": 64, "dr1": 64, "dr2": 64, "dr3": 64, "sp0": 64, "sp1": 64, "sp2": 64, "sp3": 64,
+    "me0": 64, "me1": 64, "me2": 96, "me3": 64, "me4": 32,
+    "v0": 64, "fm1": 64, "fm2": 96, "fm3": 64, "fm4": 32, "v1": 64, "v2": 64, "v3": 64, "v4": 8,
+    "in1": 64, "ma1": 64, "eq1": 96, "pr1": 96, "sl1": 96, "in3": 64, "ma3": 64, "eq3": 96, "pr3": 96, "sl3": 96,
+    "bv": 64, "q1": 64, "q2": 64, "q3": 64, "e2": 8, "f2": 8, "out3": 64, "r1": 64, "ret": 64, "far": 8, "bf": 64, "nr32": 64,
+    "g1": 64, "g2": 64, "g3": 64, "w4": 64, "a1": 64, "a2": 64, "a3": 64, "e4": 8, "f4": 8,
+}
+for _n in _WORK:
+    SCRATCH[_n] = ("sbuf", [128, _WORK[_n]], F32)
 
-SEMAPHORES = ["v", "a", "mm", "gi", "sdm", "sw", "sx", "scp", "sy", "al", "aw", "ar1", "ar3", "loc"]
+SEMAPHORES = ["v", "a", "mm", "gi", "sdm", "sw", "sxa", "sxb", "scp", "sy", "al", "aw", "ar1", "ar3", "loc"]
 
 ADD, SUB, MUL, MIN = AluOpType.add, AluOpType.subtract, AluOpType.mult, AluOpType.min
 LT, GT, EQ = AluOpType.is_lt, AluOpType.is_gt, AluOpType.is_equal
 AND, SHR = AluOpType.bitwise_and, AluOpType.logical_shift_right
 COPY = ActivationFunctionType.Copy
+
+T_WAKE, T_CYC = 0.08, 0.001
+T_EXT = {"gi": 1.2, "sw": 3.4, "sxa": 5.0, "al": 6.0, "aw": 9.0, "sxb": 10.5, "scp": 11.5, "ar1": 14.5, "ar3": 18.5, "mm": 19.5}
+
+
+def R(name, a, b, step=1):
+    return (name, a, b, step)
 
 
 def rank_program(g, core, T, topo):
@@ -73,18 +68,26 @@ def rank_program(g, core, T, topo):
     cores = T.cores
     pair = r // 2
     base, e = 2 * pair, r % 2
+    mate = base + 1 - e
     mid = pair == 1
     vec = g.vector
     S = T.sem
 
     near = None if mid else (0 if pair == 0 else 1)
-    NB = slice(0, 40) if mid else slice(32 * near, 32 * near + 8)
+    far = None if mid else 1 - near
+    nb = (0, 40) if mid else (32 * near, 32 * near + 8)
     low = 0 if mid else 1
     mine = low if e == 0 else 1 - low
-    far = None if mid else 1 - near
+
+    def N(name):
+        return R(name, nb[0], nb[1])
 
     def blk(name, b):
-        return T[name][:, 32 * b:32 * b + 8]
+        return R(name, 32 * b, 32 * b + 8)
+
+    def ap(o):
+        name, a, b, step = o
+        return T[name][:, a:b] if step == 1 else T[name][:, a:b:step]
 
     def sender(s, q):
         for m in (2 * s, 2 * s + 1):
@@ -95,258 +98,365 @@ def rank_program(g, core, T, topo):
     def peers(s):
         return [q for q in (2 * s, 2 * s + 1) if sender(pair, q) == r]
 
-    n_off = len(topo.engines(core, cores[base + 1 - e]))
+    n_off = len(topo.engines(core, cores[mate]))
 
     def addr(q):
         rid, pid, _ = topo.addr(cores[q])
         return rid, pid
 
-    st = {"v": 0, "vw": 0, "a": 0, "aw": 0, "loc": 0}
+    ops = []
 
-    def V(call, args, deps=()):
-        need = max([0] + list(deps))
-        if need > st["vw"]:
-            vec.wait_ge(S.v, need)
-            st["vw"] = need
+    def note(call, args, reads, writes, cost, ext=(), tail=0.0):
+        ops.append((call, args, reads, writes, tuple(ext), max(64, cost) * T_CYC, tail))
+        return len(ops) - 1
+
+    def val(x):
+        return ap(x) if isinstance(x, tuple) else x
+
+    def width(o):
+        return len(range(o[1], o[2], o[3]))
+
+    def ts(out, in0, s1, op0, s2=None, op1=None, ext=()):
+        args = (ap(out), ap(in0), val(s1), None, op0) if op1 is None else (ap(out), ap(in0), val(s1), val(s2), op0, op1)
+        return note(vec.tensor_scalar, args, [x for x in (in0, s1, s2) if isinstance(x, tuple)], [out], width(out), ext)
+
+    def tt(out, a, b, op, ext=()):
+        return note(vec.tensor_tensor, (ap(out), ap(a), ap(b), op), [a, b], [out], 2 * width(out), ext)
+
+    def ti(out, win, off, b, op):
+        return note(vec.tensor_tensor, (ap(out), ap(win).indirect(ap(off)), ap(b), op), [win, off, b], [out], 60 + 1.5 * width(out))
+
+    def tr(out, a):
+        return note(vec.transpose, (ap(out), ap(a)), [a], [out], width(out))
+
+    def scan(out, d0, d1):
+        return note(vec.tensor_tensor_scan, (ap(out), ap(d0), ap(d1), 0.0, MUL, ADD), [d0, d1], [out], width(out))
+
+    def cp(out, a):
+        return note(vec.tensor_copy, (ap(out), ap(a)), [a], [out], width(out))
+
+    def fill(name, v, a=0, b=None):
+        o = R(name, a, _WORK[name] if b is None else b)
+        return note(vec.memset, (ap(o), v), [], [o], width(o))
+
+    def quant(c, s, src, ext):
+        return note(vec.quantize_mx, (ap(c), ap(s), ap(src)), [], [c, s], 12 + 0.22 * width(src), ext)
+
+    picks = {}
+
+    def pick(key, dst, src, wid, off, n, ext, tail=0.0):
+        o = R(off, 0, n)
+        d, w = R(dst + "c", 0, 16 * n), R(src + "c", 0, wid)
+        i = note(vec.tensor_copy, (ap(d).bitcast(dt.uint32), ap(w).bitcast(dt.uint32).indirect(ap(o))), [w, o], [d], 60 + 1.5 * 16 * n, ext, tail)
+        picks[key] = (i, dst, src, wid, off, n, ext)
+        return i
+
+    fill("z32", 0.0)
+    fill("gd", 0.0)
+    fill("xx", 0.0)
+    fill("kq", 0.0, 256, 272)
+    for n in ("sp0", "sp1", "sp2", "sp3", "out3", "v2"):
+        fill(n, 0.0)
+    if not mid:
+        fill("me2", 0.0)
+    fill("base1", float(OWN - PC), 0, 32)
+    fill("base1", float(OWN + BLK - PC), 32, 64)
+    fill("base3", float(W1 - PC), 0, 32)
+    fill("base3", float(W1 + (BLK if mid else 0) - PC), 32, 64)
+    gi = [("gi", 4)]
+    P = lambda c: R("pi", c, c + 1)
+    F = lambda c: R("pf", c, c + 1)
+    ts(P(1), P(0), 15, AND, ext=gi)
+    ts(P(2), P(0), 7, AND, ext=gi)
+    ts(P(3), P(0), 3, AND, ext=gi)
+    ts(P(4), P(0), 2, SHR, 3, AND, ext=gi)
+    ts(R("g40", 0, 64), R("mod32", 0, 64), 1.0, MIN, ext=gi)
+    ts(R("g96", 0, 96), R("mod8", 0, 96), 1.0, MIN, ext=gi)
+    cp(F(0), P(1))
+    cp(F(2), P(2))
+    cp(F(3), P(3))
+    ts(F(4), P(4), 18.0, MUL)
+    ts(F(1), F(0), 16.0, ADD)
+    tt(F(5), F(4), F(3), ADD)
+    ts(R("k32p", 0, 32), R("z32", 0, 32), F(2), ADD, float(PC), MUL)
+    ts(R("rep", 0, 3), R("z32", 0, 3), F(2), ADD)
+    ts(R("rep", 3, 9), R("z32", 0, 6), F(2), ADD, 32.0, ADD)
+    for o in range(2):
+        for t in range(1, RD):
+            half, t1 = (0, t) if t <= 2 else (1, t - 2)
+            ts(R("klist", 4 * o + t - 1, 4 * o + t), F(5), float(64 * (2 * half + o) + LC * (t % 2) + 3 * t1), ADD)
+
+    my = (8 * PC * e, 8 * PC * (e + 1))
+    i_w = quant(R("p1c", *my), R("p1s", *my), R("wt", 0, 1024), [("sw", 16)])
+    quant(R("p2c", *my), R("p2s", *my), R("wt", 0, 1024), [("sw", 16)])
+    quant(R("xqc", 0, 128 * XA), R("xqs", 0, 128 * XA), R("xt", 0, 512 * XA), [("sxa", 16)])
+    i_xb = quant(R("xqc", 128 * XA, 128 * RD), R("xqs", 128 * XA, 128 * RD), R("xt", 512 * XA, 512 * RD), [("sxb", 16)])
+
+    tt(R("gd", 0, 5 * LC), R("lst", 0, 5 * LC), R("lst", LC, 6 * LC), SUB, [("sdm", 128), ("al", (NR - 1) * n_off)])
+    tr(R("xx", 0, 64), R("gd", 0, 64))
+    for q in range(4):
+        tr(R("kq", 64 * q, 64 * q + 64), R("xx", 8 * q, 8 * q + 64))
+    E = lambda a, b: R("rec", a, b)
+    O = lambda a, b: R("rec", 64 + a, 64 + b)
+
+    def widen(me, b, key):
+        return ts(R(me, 32 * b, 32 * b + 32), R("z32", 0, 32), key, LT)
+
+    def steps(t, a, b, first, count, mk):
+        for c in range(count):
+            ts(R("sp%d" % t, a + c, b, 4), R("dr%d" % t, a + c, b, 4), R("mk", mk + c, mk + c + 1), MUL)
+
+    tt(R("dk0", 0, 3), R("kq", 64, 103, 19), R("kq", 0, 39, 19), SUB)
+    note(vec.tensor_copy, (ap(R("rec", 0, 128)), ap(R("kq", 0, 272)).indirect(ap(R("klist", 0, 8)))), [R("kq", 0, 272), R("klist", 0, 8)], [R("rec", 0, 128)], 60 + 1.5 * 128)
+    ts(R("mk", 0, 3), R("dk0", 0, 3), 0.0, GT)
+    tt(R("dr0", 0, 64), O(0, 64), E(0, 64), SUB)
+    steps(0, 0, 64, 0, 3, 0)
+    tt(E(0, 64), E(0, 64), R("sp0", 0, 64), ADD)
+    tt(O(0, 64), O(0, 64), R("sp0", 0, 64), SUB)
+    ts(R("m256", 0, 1), R("dk0", pair, pair + 1), 0.0, GT, 8.0 * PC, MUL)
+    ts(R("me0", 32 * low, 32 * low + 32), R("k32p", 0, 32), R("m256", 0, 1), ADD)
+    ts(R("me0", 32 - 32 * low, 64 - 32 * low), R("k32p", 0, 32), R("m256", 0, 1), SUB, 8.0 * PC, ADD)
+    i_v0 = tr(R("v0", 0, 64), R("me0", 0, 64))
+    tt(R("dr1", 0, 63), E(1, 64), O(0, 63), SUB)
+    for b in range(2):
+        widen("me1", b, R("dr1", 5 * b, 5 * b + 1))
+    tr(R("fm1", 0, 64), R("me1", 0, 64))
+    ts(R("mk", 4, 6), R("dr1", 0, 6, 5), 0.0, GT)
+    steps(1, 16, 63, 0, 2, 4)
+    tt(O(16, 63), O(16, 63), R("sp1", 16, 63), ADD)
+    tt(E(17, 64), E(17, 64), R("sp1", 16, 63), SUB)
+
+    def lanes(i, fm, src, blocks):
+        inc, ma, eq, pr, sl, off = ["%s%d" % (n, i) for n in ("in", "ma", "eq", "pr", "sl", "off")]
+        nn = 48 * len(blocks)
+        rc = (0, 6) if len(blocks) == 2 else ((0, 3) if blocks[0] == 0 else (6, 9))
+        rep = R("rep", *rc)
+        scan(R(inc, 0, 40), R("g40", 0, 40), R(fm, 0, 40))
+        tt(R(ma, 0, 40), R(fm, 0, 40), R(src, 0, 40), MUL)
+        ti(R(eq, 0, nn), R(inc, 0, 40), rep, R("n96", 0, nn), EQ)
+        ti(R(pr, 0, nn), R(ma, 0, 40), rep, R(eq, 0, nn), MUL)
+        scan(R(sl, 0, nn), R("g96", 0, nn), R(pr, 0, nn))
+        cols = 12 * len(blocks)
+        ts(R(off, 0, cols, 2), R(sl, 7, nn, 8), F(0), ADD)
+        ts(R(off, 1, cols, 2), R(sl, 7, nn, 8), F(1), ADD)
+
+    near_blocks = [0, 1] if mid else [near]
+    lanes(1, "fm1", "v0", near_blocks)
+    aw = [("aw", 2 * n_off)]
+    pick("snd1", "snd1", "p1", OWN, "off1", 22 if mid else 10, aw, 9.0)
+    tt(N("bv"), N("base1"), N("v0"), SUB)
+    ts(N("q1"), N("in1"), float(PC), MUL)
+    tt(N("q2"), N("q1"), N("bv"), ADD)
+    tt(N("q3"), N("fm1"), N("q2"), MUL)
+    tt(N("v1"), N("v0"), N("q3"), ADD)
+    tt(R("dr2", 16, 64), O(16, 64), E(16, 64), SUB)
+    for b, c in ([(0, 0), (1, 2), (2, 1)] if mid else [(near, 1), (2, pair)]):
+        widen("me2", b, R("dr2", 16 + 5 * c, 17 + 5 * c))
+    tr(R("fm2", 0, 96), R("me2", 0, 96))
+    ts(R("mk", 8, 11), R("dr2", 16, 27, 5), 0.0, GT)
+    steps(2, 32, 64, 0, 3, 8)
+    tt(E(32, 64), E(32, 64), R("sp2", 32, 64), ADD)
+    tt(O(32, 64), O(32, 64), R("sp2", 32, 64), SUB)
+    V1 = [blk("v1" if mid or b == near else "v0", b) for b in range(2)]
+    tt(R("e2", 0, 8), V1[1], V1[0], SUB)
+    tt(R("f2", 0, 8), R("fm2", 64, 72), R("e2", 0, 8), MUL)
+    tt(blk("v2", 0), V1[0], R("f2", 0, 8), ADD)
+    tt(blk("v2", 1), V1[1], R("f2", 0, 8), SUB)
+    tt(R("dr3", 32, 63), E(33, 64), O(32, 63), SUB)
+    for b in range(2):
+        widen("me3", b, R("dr3", 32 + 5 * b, 33 + 5 * b))
+    tr(R("fm3", 0, 64), R("me3", 0, 64))
+    if not mid:
+        cp(blk("out3", far), blk("v0", near))
+    ts(N("out3"), N("v2"), float(OWN - PC), MIN)
+    lanes(3, "fm3", "out3", [0, 1])
+    pick("snd3", "snd3", "p1", OWN, "off3", 22, aw, 7.5)
+    ts(R("mk", 12, 14), R("dr3", 32, 38, 5), 0.0, GT)
+    steps(3, 48, 63, 0, 2, 12)
+    tt(O(48, 63), O(48, 63), R("sp3", 48, 63), ADD)
+    tt(E(49, 64), E(49, 64), R("sp3", 48, 63), SUB)
+    tt(N("r1"), N("fm1"), N("fm2"), MUL)
+    tt(N("ret"), N("fm1"), N("r1"), SUB)
+    if mid:
+        bf = N("base3")
+    else:
+        tt(R("far", 0, 8), blk("fm1", far), blk("fm2", near), MUL)
+        ts(N("bf"), R("far", 0, 8), float(BLK), MUL, float(W1 - PC), ADD)
+        bf = N("bf")
+    ts(N("nr32"), N("ret"), float(-PC), MUL, float(PC), ADD)
+    tt(N("g1"), N("v0"), bf, SUB)
+    tt(N("g2"), N("ret"), N("g1"), MUL)
+    tt(N("g3"), bf, N("v2"), SUB)
+    tt(N("w4"), N("g2"), N("g3"), ADD)
+    tt(N("a1"), N("nr32"), N("in3"), MUL)
+    tt(N("a2"), N("a1"), N("w4"), ADD)
+    tt(N("a3"), N("fm3"), N("a2"), MUL)
+    tt(N("v3"), N("v2"), N("a3"), ADD)
+    kc = 48 + 5 * pair
+    tt(R("d4", 0, 1), O(kc, kc + 1), E(kc, kc + 1), SUB)
+    widen("me4", 0, R("d4", 0, 1))
+    tr(R("fm4", 0, 32), R("me4", 0, 32))
+    V3 = [blk("v3" if mid or b == near else "v2", b) for b in range(2)]
+    tt(R("e4", 0, 8), V3[1], V3[0], SUB)
+    tt(R("f4", 0, 8), R("fm4", 0, 8), R("e4", 0, 8), MUL)
+    tt(R("v4", 0, 8), V3[mine], R("f4", 0, 8), ADD if mine == 0 else SUB)
+    where = [blk("v0", mine), V1[mine], blk("v2", mine), V3[mine], R("v4", 0, 8)]
+    n_in1 = sum(2 * (n_off // 2 if s == 1 else n_off) for s in ([0, 2] if mid else [1]))
+    n_in3 = 2 * 2 * (n_off // 2)
+    ext = [aw, [("scp", 32), ("ar1", n_in1)], [("scp", 32), ("ar1", n_in1)], [("ar3", n_in3)], [("ar3", n_in3)]]
+    for t in range(RD):
+        ts(R("of%d" % t, 0, 16, 2), where[t], F(0), ADD)
+        ts(R("of%d" % t, 1, 16, 2), where[t], F(1), ADD)
+        pick(t, "st%d" % t, "p1" if t == 0 else "p2", (OWN, W1, W1, W3, W3)[t], "of%d" % t, 16, ext[t], 2.5)
+
+    def out_of(t, h):
+        bank, c = 512 * ((2 * t + h) % 8), 256 * t + 128 * h
+        return T.yb[:, c:c + 128], T.ps[:, bank:bank + 128]
+    i_ev = {}
+    for t in (3, 4):
+        i_ev[t] = note(vec.tensor_copy, out_of(t, 0), [R("st%dc" % t, 0, 1)], [R("yb", 256 * t, 256 * t + 128)], 128, [("mm", 2 * t + 1)], 2.0)
+
+    n_ops = len(ops)
+    raw = [set() for _ in ops]
+    seq = [set() for _ in ops]
+    hist = {}
+    for i, (call, args, reads, writes, ex, cost, tail) in enumerate(ops):
+        for kind, regs in (("r", reads), ("w", writes)):
+            for name, a, b, step in regs:
+                cols = set(range(a, b, step))
+                for j, k2, c2 in hist.get(name, []):
+                    if j != i and (kind == "w" or k2 == "w") and not cols.isdisjoint(c2):
+                        (raw if k2 == "w" else seq)[i].add(j)
+        for kind, regs in (("r", reads), ("w", writes)):
+            for name, a, b, step in regs:
+                hist.setdefault(name, []).append((i, kind, set(range(a, b, step))))
+    prio = [0.0] * n_ops
+    for i in range(n_ops - 1, -1, -1):
+        prio[i] += ops[i][5] + ops[i][6]
+        for j in raw[i]:
+            prio[j] = max(prio[j], prio[i] + T_WAKE)
+        for j in seq[i]:
+            prio[j] = max(prio[j], prio[i])
+    done, tok, now = {}, {}, 0.0
+    while len(tok) < n_ops:
+        best = None
+        for i in range(n_ops):
+            if i in tok or not all(j in tok for j in raw[i]) or not all(j in tok for j in seq[i]):
+                continue
+            at = max([now] + [done[j] + T_WAKE for j in raw[i]] + [T_EXT.get(s, 0.0) for s, _ in ops[i][4]])
+            if best is None or (at, -prio[i]) < best[:2]:
+                best = (at, -prio[i], i)
+        i = best[2]
+        now = done[i] = best[0] + ops[i][5]
+        tok[i] = len(tok) + 1
+    waited = {}
+
+    def vwait(sem, n):
+        if waited.get(sem, 0) < n:
+            vec.wait_ge(S[sem], n)
+            waited[sem] = n
+
+    for i in sorted(range(n_ops), key=lambda k: tok[k]):
+        call, args, reads, writes, ex, cost, tail = ops[i]
+        for sem, n in ex:
+            vwait(sem, n)
+        vwait("v", max([0] + [tok[j] for j in raw[i]]))
         call(*args).then_inc(S.v, 1)
-        st["v"] += 1
-        return st["v"]
 
-    def ts(out, in0, s1, op0, deps=(), s2=None, op1=None):
-        if op1 is None:
-            return V(vec.tensor_scalar, (out, in0, s1, None, op0), deps)
-        return V(vec.tensor_scalar, (out, in0, s1, s2, op0, op1), deps)
-
-    def tt(out, a, b, op, deps=()):
-        return V(vec.tensor_tensor, (out, a, b, op), deps)
-
-    def tr(out, a, deps=()):
-        return V(vec.transpose, (out, a), deps)
-
-    def scan(out, d0, d1, deps=()):
-        return V(vec.tensor_tensor_scan, (out, d0, d1, 0.0, MUL, ADD), deps)
-
-    mycol = T.lst[:, LC * r:LC * r + LC]
     for b in range(4):
         for h, q in ((0, g.sync), (1, g.scalar)):
             p0 = 32 * b + 16 * h
             q.dma_start(T.lst[p0:p0 + 16, LC * r:LC * r + LC], T.dm[:, 6 * h:6 * h + LC]).then_inc(S.sdm, 16)
     g.sync.dma_start(T.wt[:], T.w[:]).then_inc(S.sw, 16)
+    g.sync.dma_start(T.xt[:, 0:512 * XA], T.x[:, 0:512 * XA]).then_inc(S.sxa, 16)
+    g.sync.wait_ge(S.v, tok[i_v0])
+    g.sync.dma_start(T.xt[:, 512 * XA:], T.x[:, 512 * XA:]).then_inc(S.sxb, 16)
+    his = slice(8 * PC * (1 - e), 8 * PC * (2 - e))
+    g.sync.wait_ge(S.aw, 2 * n_off)
+    g.sync.dma_start(T.p2c[:, his].bitcast(dt.uint8), T.p1c[:, his].bitcast(dt.uint8)).then_inc(S.scp, 16)
+    g.sync.dma_start(T.p2s[:, his], T.p1s[:, his]).then_inc(S.scp, 16)
 
+    acount, asem, swaited = [0], {}, {}
+
+    def swait(sem, n):
+        if swaited.get(sem, 0) < n:
+            g.scalar.wait_ge(S[sem], n)
+            swaited[sem] = n
+
+    def scales(key):
+        i, dst, src, wid, off, n, ex = picks[key]
+        for sem, c in ex:
+            swait(sem, c)
+        swait("v", max([0] + [tok[j] for j in raw[i]]))
+        g.scalar.activation(T[dst + "s"][:, 0:16 * n], T[src + "s"][:, 0:wid].indirect(T[off][:, 0:n]), COPY).then_inc(S.a, 1)
+        acount[0] += 1
+        asem[key] = acount[0]
+
+    def evac(t, h):
+        swait("mm", 2 * t + h + 1)
+        g.scalar.activation(*out_of(t, h), COPY).then_inc(S.a, 1)
+        acount[0] += 1
+        asem["y%d" % t] = acount[0]
+
+    for key in sorted(("snd1", "snd3", 0), key=lambda k: tok[picks[k][0]]):
+        scales(key)
+    evac(0, 0)
+    evac(0, 1)
+    scales(1)
+    scales(2)
+    for t in (1, 2):
+        evac(t, 0)
+        evac(t, 1)
+    scales(3)
+    scales(4)
+    evac(3, 1)
+    evac(4, 1)
+
+    big = {"allow_small_or_imprecise_dtypes": True}
     g.iota(T.pi[:, 0:1], [[0, 1]], 0, 1).then_inc(S.gi, 1)
-    g.iota(T.k32[:], [[0, 2], [32, 32]], 0, 0, allow_small_or_imprecise_dtypes=True).then_inc(S.gi, 1)
-    g.iota(T.kk[:], [[0, 2], [1, 32]], 0, 0, allow_small_or_imprecise_dtypes=True).then_inc(S.gi, 1)
-    g.iota(T.pr1[:], [[0, 12], [1, 8]], 0, 0, allow_small_or_imprecise_dtypes=True).then_inc(S.gi, 1)
-    g.iota(T.n96[:], [[0, 2], [1, 6], [0, 8]], 1, 0, allow_small_or_imprecise_dtypes=True).then_inc(S.gi, 1)
-
-    def fill(name, val, cols=None):
-        ap = T[name][:] if cols is None else T[name][:, cols]
-        return V(vec.memset, (ap, val))
-    fill("z32", 0.0)
-    fill("gd", 0.0)
-    fill("xx", 0.0)
-    fill("kq", 0.0, slice(256, 272))
-    for n in ("st0", "st1", "st2", "st3", "v0", "out3"):
-        fill(n, 0.0)
-    if not mid:
-        fill("me2", 0.0)
-    fill("base1", float(OWN - PC), slice(0, 32))
-    fill("base1", float(OWN + BLK - PC), slice(32, 64))
-    fill("base3", float(W1 - PC), slice(0, 32))
-    tf = fill("base3", float(W1 + (BLK if mid else 0) - PC), slice(32, 64))
-    vec.wait_ge(S.gi, 5)
-    P = T.pi
-    c15 = ts(P[:, 1:2], P[:, 0:1], 15, AND)
-    c7 = ts(P[:, 2:3], P[:, 0:1], 7, AND)
-    c3 = ts(P[:, 3:4], P[:, 0:1], 3, AND)
-    ch = ts(P[:, 4:5], P[:, 0:1], 2, SHR, (), 3, AND)
-    ts(T.g40[:], T.kk[:], 1.0, MIN)
-    tg = ts(T.g96[:], T.pr1[:], 1.0, MIN)
-    F = T.pf
-    f15 = V(vec.tensor_copy, (F[:, 0:1], P[:, 1:2]), (c15,))
-    f7 = V(vec.tensor_copy, (F[:, 2:3], P[:, 2:3]), (c7,))
-    f3 = V(vec.tensor_copy, (F[:, 3:4], P[:, 3:4]), (c3,))
-    fh = ts(F[:, 4:5], P[:, 4:5], 18.0, MUL, (ch,))
-    ts(F[:, 1:2], F[:, 0:1], 16.0, ADD, (f15,))
-    ts(T.kk[:], T.k32[:], 256.0, ADD, (tg,))
-    fv = tt(F[:, 5:6], F[:, 4:5], F[:, 3:4], ADD, (fh, f3))
-    ts(T.rep[:, 0:3], T.z32[:, 0:3], F[:, 2:3], ADD, (f7,))
-    ts(T.rep[:, 3:9], T.z32[:, 0:6], F[:, 2:3], ADD, (f7,), 32.0, ADD)
-    for o in range(2):
-        for t in range(1, RD):
-            half, t1 = (0, t) if t <= 2 else (1, t - 2)
-            tc = ts(T.klist[:, 4 * o + t - 1:4 * o + t], F[:, 5:6], float(64 * (2 * half + o) + LC * (t % 2) + 3 * t1), ADD, (fv,))
-
-    g.wait_ge(S.sdm, 128)
+    g.iota(T.mod32[:], [[0, 2], [1, 32]], 0, 0, **big).then_inc(S.gi, 1)
+    g.iota(T.mod8[:], [[0, 12], [1, 8]], 0, 0, **big).then_inc(S.gi, 1)
+    g.iota(T.n96[:], [[0, 2], [1, 6], [0, 8]], 1, 0, **big).then_inc(S.gi, 1)
+    left = [0]
     others = [q for q in range(NR) if q != r]
+    mycol = T.lst[:, LC * r:LC * r + LC]
+    g.wait_ge(S.sdm, 128)
     g.remote_dma_fused([RemoteDMATransfer(
         dst_ids=[DstId(rid=addr(q)[0], pnc=addr(q)[1]) for q in others], dma_engine_mask=topo.mask(core, cores[others[0]]),
         remote_sem=S.al, srcs=[mycol], dsts=[mycol] * len(others))], local_sem=S.loc)
-    st["loc"] += n_off
-
-    vec.wait_ge(S.sw, 16)
-    my = slice(8 * PC * e, 8 * PC * (e + 1))
-    tw = V(vec.quantize_mx, (T.p1c[:, my], T.p1s[:, my], T.wt[:]))
-    g.wait_ge(S.v, tw)
-    mate = base + 1 - e
+    left[0] += n_off
+    g.wait_ge(S.v, tok[i_w])
+    mys = slice(*my)
     rid, pid = addr(mate)
     mk = topo.mask(core, cores[mate])
-    g.remote_dma(T.p1c[:, my].bitcast(dt.uint8), T.p1c[:, my].bitcast(dt.uint8), S.aw, S.loc, pid, rid, mk)
-    g.remote_dma(T.p1s[:, my], T.p1s[:, my], S.aw, S.loc, pid, rid, mk)
-    st["loc"] += 2 * n_off
-    g.sync.wait_ge(S.v, tw)
-    g.sync.dma_start(T.xt[:], T.x[:]).then_inc(S.sx, 16)
+    g.remote_dma(T.p1c[:, mys].bitcast(dt.uint8), T.p1c[:, mys].bitcast(dt.uint8), S.aw, S.loc, pid, rid, mk)
+    g.remote_dma(T.p1s[:, mys], T.p1s[:, mys], S.aw, S.loc, pid, rid, mk)
+    left[0] += 2 * n_off
 
-    vec.wait_ge(S.sdm, 128)
-    vec.wait_ge(S.al, (NR - 1) * n_off)
-    k = tt(T.gd[:, 0:5 * LC], T.lst[:, 0:5 * LC], T.lst[:, LC:6 * LC], SUB, (tf,))
-    k = tr(T.xx[:, 0:64], T.gd[:], (k,))
-    for q in range(4):
-        kq = tr(T.kq[:, 64 * q:64 * q + 64], T.xx[:, 8 * q:8 * q + 64], (k,))
-    E0, O0 = 0, 64
-    E = lambda a, b: T.rec[:, E0 + a:E0 + b]
-    O = lambda a, b: T.rec[:, O0 + a:O0 + b]
-
-    def widen(me, b, key, deps):
-        return ts(T[me][:, 32 * b:32 * b + 32], T.z32[:], key, LT, deps)
-
-    d = tt(T.dk0[:, 0:3], T.kq[:, 64:103:19], T.kq[:, 0:39:19], SUB, (kq,))
-    kr = V(vec.tensor_copy, (T.rec[:], T.kq[:].indirect(T.klist[:])), (kq, tc))
-    m = ts(T.mk[:, 0:3], T.dk0[:, 0:3], 0.0, GT, (d,))
-    w0 = widen("me0", 0, T.dk0[:, pair:pair + 1], (d,))
-    d = tt(T.dr0[:], O(0, 64), E(0, 64), SUB, (kr,))
-    x0 = tr(T.fm0[:], T.me0[:], (w0,))
-    for c in range(3):
-        s = ts(T.st0[:, c:64:4], T.dr0[:, c:64:4], T.mk[:, c:c + 1], MUL, (d, m))
-    u1 = tt(E(0, 64), E(0, 64), T.st0[:], ADD, (s,))
-    u2 = tt(O(0, 64), O(0, 64), T.st0[:], SUB, (s,))
-    t1 = ts(T.tm[:], T.fm0[:, 0:8], 256.0, MUL, (x0,))
-    d1 = tt(T.dr1[:, 0:63], E(1, 64), O(0, 63), SUB, (u2,))
-    vl = tt(blk("v0", low), T.tm[:], T.k32[:, 0:8], ADD, (t1,))
-    w1 = [widen("me1", b, T.dr1[:, 5 * b:5 * b + 1], (d1,)) for b in range(2)]
-    v0 = tt(blk("v0", 1 - low), T.kk[:, 0:8], T.tm[:], SUB, (t1,))
-    x1 = tr(T.fm1[:], T.me1[:], (w1[1],))
-    m1 = ts(T.mk[:, 4:6], T.dr1[:, 0:6:5], 0.0, GT, (d1,))
-
-    def lanes(i, fm, src, blocks, fillers):
-        inc, ma, eq, pr, sc, off = ["%s%d" % (n, i) for n in ("in", "ma", "eq", "pr", "sc", "off")]
-        if i == 1:
-            sc = "sc1"
-        nn = 48 * len(blocks)
-        rc = (0, 6) if len(blocks) == 2 else ((0, 3) if blocks[0] == 0 else (6, 9))
-        rep = T.rep[:, rc[0]:rc[1]]
-        fillers = list(fillers)
-
-        def fl():
-            if fillers:
-                fillers.pop(0)()
-        ti = scan(T[inc][:, 0:40], T.g40[:, 0:40], T[fm][:, 0:40], (x1 if i == 1 else x3[0],))
-        tm = tt(T[ma][:, 0:40], T[fm][:, 0:40], T[src][:, 0:40], MUL, (v0 if i == 1 else x3[1],))
-        q = tt(T[eq][:, 0:nn], T[inc][:, 0:40].indirect(rep), T.n96[:, 0:nn], EQ, (ti,))
-        fl()
-        q = tt(T[pr][:, 0:nn], T[ma][:, 0:40].indirect(rep), T[eq][:, 0:nn], MUL, (q, tm))
-        fl()
-        q = scan(T[sc][:, 0:nn], T.g96[:, 0:nn], T[pr][:, 0:nn], (q,))
-        fl()
-        fl()
-        cols = 12 * len(blocks)
-        ts(T[off][:, 0:cols:2], T[sc][:, 7:nn:8], F[:, 0:1], ADD, (q,))
-        q = ts(T[off][:, 1:cols:2], T[sc][:, 7:nn:8], F[:, 1:2], ADD, (q,))
-        return ti, q
-
-    def pick(dst_c, dst_s, src_c, src_s, width, off, n, deps, waits):
-        for sem, val in waits:
-            vec.wait_ge(sem, val)
-            g.scalar.wait_ge(sem, val)
-        q = V(vec.tensor_copy, (T[dst_c][:, 0:16 * n].bitcast(dt.uint32), T[src_c][:, 0:width].bitcast(dt.uint32).indirect(T[off][:, 0:n])), deps)
-        g.scalar.wait_ge(S.v, max(deps))
-        g.scalar.activation(T[dst_s][:, 0:16 * n], T[src_s][:, 0:width].indirect(T[off][:, 0:n]), COPY).then_inc(S.a, 1)
-        st["a"] += 1
-        return q, st["a"]
-
-    def send(i, jobs, pk):
-        sem = S["ar%d" % i]
-        g.wait_ge(S.v, pk[0])
+    def send(i, jobs):
+        key = "snd%d" % i
+        g.wait_ge(S.v, tok[picks[key][0]])
         eng = topo.engines(core, cores[jobs[0][1]])
         per = len(eng) // len(jobs)
         for kind in ("c", "s"):
             if kind == "s":
-                g.wait_ge(S.a, pk[1])
-            sb, pb = T["snd%d%s" % (i, kind)], T["p2%s" % kind]
+                g.wait_ge(S.a, asem[key])
             trs = []
             for n, (a, q, p) in enumerate(jobs):
-                mask = sum(1 << x for x in eng[per * n:per * n + per])
-                src, dst = sb[:, a:a + BLK], pb[:, p:p + BLK]
+                src, dst = T[key + kind][:, a:a + BLK], T["p2" + kind][:, p:p + BLK]
                 if kind == "c":
                     src, dst = src.bitcast(dt.uint8), dst.bitcast(dt.uint8)
-                trs.append(RemoteDMATransfer(dst_ids=[DstId(rid=addr(q)[0], pnc=addr(q)[1])], dma_engine_mask=mask,
-                                             remote_sem=sem, srcs=[src], dsts=[dst]))
+                trs.append(RemoteDMATransfer(dst_ids=[DstId(rid=addr(q)[0], pnc=addr(q)[1])], srcs=[src], dsts=[dst],
+                                             dma_engine_mask=sum(1 << x for x in eng[per * n:per * n + per]), remote_sem=S["ar%d" % i]))
             g.remote_dma_fused(trs, local_sem=S.loc)
-            st["loc"] += per * len(jobs)
+            left[0] += per * len(jobs)
 
-    hold = {}
-
-    def f_step1a():
-        hold["a"] = ts(T.st1[:, 16:63:4], T.dr1[:, 16:63:4], T.mk[:, 4:5], MUL, (m1,))
-
-    def f_step1b():
-        hold["b"] = ts(T.st1[:, 17:63:4], T.dr1[:, 17:63:4], T.mk[:, 5:6], MUL, (m1,))
-
-    def f_o1():
-        hold["o"] = tt(O(16, 63), O(16, 63), T.st1[:, 16:63], ADD, (hold["b"],))
-
-    def f_e1():
-        hold["e"] = tt(E(17, 64), E(17, 64), T.st1[:, 16:63], SUB, (hold["b"],))
-
-    near_blocks = [0, 1] if mid else [near]
-    ti1, to1 = lanes(1, "fm1", "v0", near_blocks, [f_step1a, f_step1b, f_o1, f_e1])
     GA = 6 * PC
-    pk1 = pick("snd1c", "snd1s", "p1c", "p1s", OWN, "off1", 22 if mid else 10, (to1,), [(S.aw, 2 * n_off)])
     jobs = []
     for n, b in enumerate(near_blocks):
-        s = pair - 1 if b == pair - 1 else pair + 1
-        for q in peers(s):
+        for q in peers(pair - 1 if b == pair - 1 else pair + 1):
             jobs.append((GA * n, q, OWN + BLK * b))
-    send(1, jobs, pk1)
-    g.sync.wait_ge(S.aw, 2 * n_off)
-    g.sync.wait_ge(S.v, pk1[0])
-    g.sync.dma_start(T.p2c[:, 0:OWN].bitcast(dt.uint8), T.p1c[:, 0:OWN].bitcast(dt.uint8)).then_inc(S.scp, 16)
-    g.sync.dma_start(T.p2s[:, 0:OWN], T.p1s[:, 0:OWN]).then_inc(S.scp, 16)
-
-    d2 = tt(T.dr2[:, 16:64], O(16, 64), E(16, 64), SUB, (hold["e"],))
-    tq = ts(T.q1[:, NB], T.in1[:, NB], 32.0, MUL, (ti1,))
-    tb = tt(T.bv[:, NB], T.base1[:, NB], T.v0[:, NB], SUB, (v0,))
-    m2 = ts(T.mk[:, 8:11], T.dr2[:, 16:27:5], 0.0, GT, (d2,))
-    order = [(0, 0), (1, 2), (2, 1)] if mid else [(near, 1), (2, pair)]
-    for b, c in order:
-        w2 = widen("me2", b, T.dr2[:, 16 + 5 * c:17 + 5 * c], (d2,))
-    tq = tt(T.q2[:, NB], T.q1[:, NB], T.bv[:, NB], ADD, (tq, tb))
-    x2 = tr(T.fm2[:], T.me2[:], (w2,))
-    for c in range(3):
-        s = ts(T.st2[:, 32 + c:64:4], T.dr2[:, 32 + c:64:4], T.mk[:, 8 + c:9 + c], MUL, (m2,))
-    tq = tt(T.q3[:, NB], T.fm1[:, NB], T.q2[:, NB], MUL, (tq,))
-    u1 = tt(E(32, 64), E(32, 64), T.st2[:, 32:64], ADD, (s,))
-    u2 = tt(O(32, 64), O(32, 64), T.st2[:, 32:64], SUB, (s,))
-    tv1 = tt(T.v1[:, NB], T.v0[:, NB], T.q3[:, NB], ADD, (tq,))
-    d3 = tt(T.dr3[:, 32:63], E(33, 64), O(32, 63), SUB, (u2,))
-    V1 = [blk("v1" if mid or b == near else "v0", b) for b in range(2)]
-    td = tt(T.e2[:], V1[1], V1[0], SUB, (tv1,))
-    for b in range(2):
-        w3 = widen("me3", b, T.dr3[:, 32 + 5 * b:33 + 5 * b], (d3,))
-    td = tt(T.f2[:], T.fm2[:, 64:72], T.e2[:], MUL, (td, x2))
-    x3t = tr(T.fm3[:], T.me3[:], (w3,))
-    m3 = ts(T.mk[:, 12:14], T.dr3[:, 32:38:5], 0.0, GT, (d3,))
-    ta = tt(blk("v2", 0), V1[0], T.f2[:], ADD, (td,))
-    tv2 = tt(blk("v2", 1), V1[1], T.f2[:], SUB, (td,))
-    if mid:
-        ts(T.out3[:, 0:8], T.v2[:, 0:8], float(OWN - PC), MIN, (ta,))
-        to3 = ts(T.out3[:, 32:40], T.v2[:, 32:40], float(OWN - PC), MIN, (tv2,))
-    else:
-        V(vec.tensor_copy, (blk("out3", far), blk("v0", near)))
-        to3 = ts(blk("out3", near), blk("v2", near), float(OWN - PC), MIN, (tv2,))
-    x3 = (x3t, max(to3, x3t))
-    ti3, tf3 = lanes(3, "fm3", "out3", [0, 1], [])
-    pk3 = pick("snd3c", "snd3s", "p1c", "p1s", OWN, "off3", 22, (tf3,), [])
+    send(1, jobs)
     jobs = []
     for b in range(2):
         if mid:
@@ -357,126 +467,20 @@ def rank_program(g, core, T, topo):
             dst, col = 2 - pair, W1 + BLK
         for q in peers(dst):
             jobs.append((GA * b, q, col))
-    send(3, jobs, pk3)
+    send(3, jobs)
 
-    def offs(t, v, deps):
-        ts(T["offs%d" % t][:, 0:16:2], v, F[:, 0:1], ADD, deps)
-        return ts(T["offs%d" % t][:, 1:16:2], v, F[:, 1:2], ADD, deps)
-
-    def tile(t, src, width, dep, waits):
-        return pick(SC_NAME[t], "ss%d" % t, src + "c", src + "s", width, "offs%d" % t, 16, (dep,), waits)
-
-    def products(t, pk, first):
-        g.tensor.wait_ge(S.v, max(pk[0], first))
-        g.tensor.wait_ge(S.a, pk[1])
-        for h in range(2):
-            bank = 512 * ((2 * t + h) % 8)
-            g.tensor.matmul_mx(T.ps[:, bank:bank + 128], T[SC_NAME[t]][:, 128 * h:128 * h + 128], T["ss%d" % t][:, 128 * h:128 * h + 128],
-                               T.xq[:, 128 * t:128 * t + 128], T.xs[:, 128 * t:128 * t + 128], True, True).then_inc(S.mm, 1)
-
-    def out_of(t, h):
-        bank = 512 * ((2 * t + h) % 8)
-        c = 256 * t + 128 * h
-        return T.yb[:, c:c + 128], T.ps[:, bank:bank + 128]
-
-    def evac_s(t, h):
-        o, i = out_of(t, h)
-        g.scalar.wait_ge(S.mm, 2 * t + h + 1)
-        g.scalar.activation(o, i, COPY).then_inc(S.a, 1)
-        st["a"] += 1
-
-    def evac_v(t, h):
-        o, i = out_of(t, h)
-        vec.wait_ge(S.mm, 2 * t + h + 1)
-        return V(vec.tensor_copy, (o, i))
-
-    def store(t, va, aa):
-        if va:
-            g.sync.wait_ge(S.v, va)
-        g.sync.wait_ge(S.a, aa)
-        g.sync.dma_start(T.y[:, 256 * t:256 * t + 256], T.yb[:, 256 * t:256 * t + 256]).then_inc(S.sy, 16)
-
-    vec.wait_ge(S.sx, 16)
-    xqt = []
     for t in range(RD):
-        xqt.append(V(vec.quantize_mx, (T.xq[:, 128 * t:128 * t + 128], T.xs[:, 128 * t:128 * t + 128], T.xt[:, 512 * t:512 * t + 512])))
-        if t == 0:
-            q = offs(0, blk("v0", mine), (v0,))
-            pk = tile(0, "p1", OWN, q, [])
-            products(0, pk, xqt[0])
-    for h in range(2):
-        evac_s(0, h)
-    store(0, 0, st["a"])
-
-    n_in1 = 0
-    for s in ([0, 2] if mid else [1]):
-        n_in1 += 2 * (n_off // 2 if s == 1 else n_off)
-    q1 = offs(1, V1[mine], (tv1,))
-    q2 = offs(2, blk("v2", mine), (ta, tv2))
-    pk = tile(1, "p2", W1, q1, [(S.scp, 32), (S.ar1, n_in1)])
-    products(1, pk, xqt[1])
-    pk = tile(2, "p2", W1, q2, [])
-    products(2, pk, xqt[2])
-    for t in (1, 2):
+        g.tensor.wait_ge(S.v, max([tok[picks[t][0]], tok[i_xb if t >= XA else i_xb - 1]]))
+        g.tensor.wait_ge(S.a, asem[t])
         for h in range(2):
-            evac_s(t, h)
-        store(t, 0, st["a"])
+            st, c = slice(128 * h, 128 * h + 128), slice(128 * t, 128 * t + 128)
+            g.tensor.matmul_mx(out_of(t, h)[1], T["st%dc" % t][:, st], T["st%ds" % t][:, st], T.xqc[:, c], T.xqs[:, c], True, True).then_inc(S.mm, 1)
 
-    a = tt(T.r1[:, NB], T.fm1[:, NB], T.fm2[:, NB], MUL, (x2,))
-    if not mid:
-        fa = tt(T.far[:], blk("fm1", far), blk("fm2", near), MUL, (x2,))
-    s = ts(T.st3[:, 48:63:4], T.dr3[:, 48:63:4], T.mk[:, 12:13], MUL, (m3,))
-    s = ts(T.st3[:, 49:63:4], T.dr3[:, 49:63:4], T.mk[:, 13:14], MUL, (m3,))
-    rt = tt(T.ret[:, NB], T.fm1[:, NB], T.r1[:, NB], SUB, (a,))
-    if mid:
-        bf = T.base3[:, NB]
-        tbf = 0
-    else:
-        tbf = ts(blk("bf", near), T.far[:], float(BLK), MUL, (fa,), float(W1 - PC), ADD)
-        bf = T.bf[:, NB]
-    uo = tt(O(48, 63), O(48, 63), T.st3[:, 48:63], ADD, (s,))
-    ue = tt(E(49, 64), E(49, 64), T.st3[:, 48:63], SUB, (s,))
-    nt = ts(T.nret[:, NB], T.ret[:, NB], -1.0, MUL, (rt,), 1.0, ADD)
-    n3 = ts(T.nr32[:, NB], T.ret[:, NB], -32.0, MUL, (rt,), 32.0, ADD)
-    wb = tt(T.w2[:, NB], T.ret[:, NB], T.v0[:, NB], MUL, (rt,))
-    kc = 48 + 5 * pair
-    d4 = tt(T.d4[:, 0:1], O(kc, kc + 1), E(kc, kc + 1), SUB, (ue,))
-    wa = tt(T.w1[:, NB], T.nret[:, NB], bf, MUL, (nt, tbf))
-    a1 = tt(T.a1[:, NB], T.nr32[:, NB], T.in3[:, NB], MUL, (n3, ti3))
-    w4 = widen("me4", 0, T.d4[:, 0:1], (d4,))
-    wc = tt(T.w3[:, NB], T.w1[:, NB], T.w2[:, NB], ADD, (wa, wb))
-    x4 = tr(T.fm4[:], T.me4[:], (w4,))
-    if mid:
-        tt(blk("w4", 0), blk("w3", 0), blk("v2", 0), SUB, (wc,))
-        wd = tt(blk("w4", 1), blk("w3", 1), blk("v2", 1), SUB, (wc,))
-        parts = [0, 1]
-    else:
-        wd = tt(blk("w4", near), blk("w3", near), blk("v2", near), SUB, (wc,))
-        parts = [near]
-    for b in parts:
-        a2 = tt(blk("a2", b), blk("a1", b), blk("w4", b), ADD, (a1, wd))
-    for b in parts:
-        a3 = tt(blk("a3", b), blk("fm3", b), blk("a2", b), MUL, (a2,))
-    for b in parts:
-        tv3 = tt(blk("v3", b), blk("v2", b), blk("a3", b), ADD, (a3,))
-    V3 = [blk("v3" if mid or b == near else "v2", b) for b in range(2)]
-    q3 = offs(3, V3[mine], (tv3,))
-    td = tt(T.e4[:], V3[1], V3[0], SUB, (tv3,))
-    td = tt(T.f4[:], T.fm4[:, 0:8], T.e4[:], MUL, (td, x4))
-    td = tt(T.v4[:], V3[mine], T.f4[:], ADD if mine == 0 else SUB, (td,))
-    q4 = offs(4, T.v4[:], (td,))
-
-    n_in3 = 2 * 2 * (n_off // 2)
-    pk = tile(3, "p2", W3, q3, [(S.ar3, n_in3)])
-    products(3, pk, xqt[3])
-    pk = tile(4, "p2", W3, q4, [])
-    g.tensor.wait_ge(S.a, 9)
-    products(4, pk, xqt[4])
-    va = evac_v(3, 0)
-    evac_s(3, 1)
-    store(3, va, st["a"])
-    va = evac_v(4, 0)
-    evac_s(4, 1)
-    store(4, va, st["a"])
+    for t in range(RD):
+        if t in i_ev:
+            g.sync.wait_ge(S.v, tok[i_ev[t]])
+        g.sync.wait_ge(S.a, asem["y%d" % t])
+        g.sync.dma_start(T.y[:, 256 * t:256 * t + 256], T.yb[:, 256 * t:256 * t + 256]).then_inc(S.sy, 16)
+    g.sync.wait_ge(S.v, n_ops)
     g.sync.wait_ge(S.sy, 16 * RD)
-    g.wait_ge(S.loc, st["loc"])
+    g.wait_ge(S.loc, left[0])

@@ -12,6 +12,7 @@ W3 = W1 + 2 * BLK
 LC = 9
 SB = 12 * PC - PC
 XA = 3
+KH = 144
 
 F32 = "float32"
 SCRATCH = {
@@ -26,35 +27,36 @@ SCRATCH = {
     "yb": ("sbuf", [128, 256 * RD], F32),
     "ps": ("psum", [128, 4096], F32),
     "pi": ("sbuf", [128, 8], "int32"),
-    "klist": ("sbuf", [128, 8], "uint16"), "rep": ("sbuf", [128, 12], "uint16"),
-    "off1": ("sbuf", [128, 24], "uint16"), "off3": ("sbuf", [128, 24], "uint16"),
+    "klist": ("sbuf", [128, 8], "uint16"), "rep": ("sbuf", [128, 12], "uint16"), "m4": ("sbuf", [128, 2], "uint16"),
+    "off1": ("sbuf", [128, 24], "uint16"), "off3": ("sbuf", [128, 24], "uint16"), "ofh": ("sbuf", [128, 16], "uint16"),
 }
 for _t in range(RD):
     SCRATCH["of%d" % _t] = ("sbuf", [128, 16], "uint16")
     SCRATCH["st%dc" % _t] = ("sbuf", [128, 256], "float8_e4m3fn_x4")
     SCRATCH["st%ds" % _t] = ("sbuf", [128, 256], "uint8")
 _WORK = {
-    "pf": 8, "z32": 32, "k32p": 32, "mod32": 64, "g40": 64, "mod8": 96, "g96": 96, "n96": 96, "base1": 64, "base3": 64,
-    "gd": 64, "xx": 96, "kq": 272, "rec": 128, "dk0": 4, "d4": 4, "mk": 16, "m256": 4,
-    "dr0": 64, "dr1": 64, "dr2": 64, "dr3": 64, "sp0": 64, "sp1": 64, "sp2": 64, "sp3": 64,
+    "pf": 8, "z32": 32, "k32p": 32, "mod16": 16, "mod32": 64, "g40": 64, "mod8": 96, "g96": 96, "n96": 96, "base1": 64, "base3": 64,
+    "gd": 64, "xx": 96, "kq": 2 * KH, "reca": 64, "recb": 64, "dk0": 4, "d4": 4, "mk": 32, "m256": 4,
+    "da0": 32, "db0": 32, "da1": 32, "db1": 32, "da2": 16, "db2": 32, "db3": 32,
+    "sa0": 32, "sb0": 32, "sa1": 32, "sb1": 32, "sb2": 32, "sb3": 32,
     "me0": 64, "me1": 64, "me2": 96, "me3": 64, "me4": 32,
     "v0": 64, "fm1": 64, "fm2": 96, "fm3": 64, "fm4": 32, "v1": 64, "v2": 64, "v3": 64, "v4": 8,
     "in1": 64, "ma1": 64, "eq1": 96, "pr1": 96, "sl1": 96, "in3": 64, "ma3": 64, "eq3": 96, "pr3": 96, "sl3": 96,
-    "bv": 64, "q1": 64, "q2": 64, "q3": 64, "e2": 8, "f2": 8, "out3": 64, "r1": 64, "ret": 64, "far": 8, "bf": 64, "nr32": 64,
-    "g1": 64, "g2": 64, "g3": 64, "w4": 64, "a1": 64, "a2": 64, "a3": 64, "e4": 8, "f4": 8,
+    "out3": 64, "e0": 8, "f0": 8, "bv": 64, "q1": 64, "q2": 64, "q3": 64, "e2": 8, "f2": 8, "r1": 64, "ret": 64, "far": 8,
+    "bf": 64, "nr32": 64, "g1": 64, "g2": 64, "g3": 64, "w4": 64, "a1": 64, "a2": 64, "a3": 64, "e4": 8, "f4": 8,
 }
 for _n in _WORK:
     SCRATCH[_n] = ("sbuf", [128, _WORK[_n]], F32)
 
-SEMAPHORES = ["v", "a", "mm", "gi", "sdm", "sw", "sxa", "sxb", "scp", "sy", "al", "aw", "ar1", "ar3", "loc"]
+SEMAPHORES = ["v", "a", "mm", "gi", "sdm", "sw", "sxa", "sxb", "sy", "al", "aw", "ar1", "ar3", "loc"]
 
 ADD, SUB, MUL, MIN = AluOpType.add, AluOpType.subtract, AluOpType.mult, AluOpType.min
 LT, GT, EQ = AluOpType.is_lt, AluOpType.is_gt, AluOpType.is_equal
 AND, SHR = AluOpType.bitwise_and, AluOpType.logical_shift_right
-COPY = ActivationFunctionType.Copy
+COPY, IDENT = ActivationFunctionType.Copy, ActivationFunctionType.Identity
 
-T_WAKE, T_CYC = 0.08, 0.001
-T_EXT = {"gi": 1.2, "sw": 3.4, "sxa": 5.0, "al": 6.0, "aw": 9.0, "sxb": 10.5, "scp": 11.5, "ar1": 14.5, "ar3": 18.5, "mm": 19.5}
+T_WAKE, T_CYC, T_PE = 0.1, 0.001, 0.3
+T_EXT = {"gi": 1.2, "sw": 3.4, "sxa": 5.0, "al": 6.0, "aw": 8.5, "sxb": 10.5, "ar1": 13.5, "ar3": 17.0}
 
 
 def R(name, a, b, step=1):
@@ -70,7 +72,7 @@ def rank_program(g, core, T, topo):
     base, e = 2 * pair, r % 2
     mate = base + 1 - e
     mid = pair == 1
-    vec = g.vector
+    vec, sca = g.vector, g.scalar
     S = T.sem
 
     near = None if mid else (0 if pair == 0 else 1)
@@ -106,8 +108,8 @@ def rank_program(g, core, T, topo):
 
     ops = []
 
-    def note(call, args, reads, writes, cost, ext=(), tail=0.0):
-        ops.append((call, args, reads, writes, tuple(ext), max(64, cost) * T_CYC, tail))
+    def note(q, call, args, reads, writes, cost, ext=(), tail=0.0, lag=0.0, kw=None):
+        ops.append((q, call, args, kw or {}, reads, writes, tuple(ext), max(64, cost) * T_CYC, tail, lag))
         return len(ops) - 1
 
     def val(x):
@@ -118,52 +120,59 @@ def rank_program(g, core, T, topo):
 
     def ts(out, in0, s1, op0, s2=None, op1=None, ext=()):
         args = (ap(out), ap(in0), val(s1), None, op0) if op1 is None else (ap(out), ap(in0), val(s1), val(s2), op0, op1)
-        return note(vec.tensor_scalar, args, [x for x in (in0, s1, s2) if isinstance(x, tuple)], [out], width(out), ext)
+        return note("v", vec.tensor_scalar, args, [x for x in (in0, s1, s2) if isinstance(x, tuple)], [out], width(out), ext)
+
+    def af(out, in0, scale, bias):
+        return note("a", sca.activation, (ap(out), ap(in0), IDENT), [x for x in (in0, scale, bias) if isinstance(x, tuple)], [out],
+                    width(out), kw={"bias": val(bias), "scale": val(scale)})
 
     def tt(out, a, b, op, ext=()):
-        return note(vec.tensor_tensor, (ap(out), ap(a), ap(b), op), [a, b], [out], 2 * width(out), ext)
+        return note("v", vec.tensor_tensor, (ap(out), ap(a), ap(b), op), [a, b], [out], 2 * width(out), ext)
 
     def ti(out, win, off, b, op):
-        return note(vec.tensor_tensor, (ap(out), ap(win).indirect(ap(off)), ap(b), op), [win, off, b], [out], 60 + 1.5 * width(out))
+        return note("v", vec.tensor_tensor, (ap(out), ap(win).indirect(ap(off)), ap(b), op), [win, off, b], [out], 50 + 1.5 * width(out))
 
     def tr(out, a):
-        return note(vec.transpose, (ap(out), ap(a)), [a], [out], width(out))
+        return note("v", vec.transpose, (ap(out), ap(a)), [a], [out], width(out))
 
     def scan(out, d0, d1):
-        return note(vec.tensor_tensor_scan, (ap(out), ap(d0), ap(d1), 0.0, MUL, ADD), [d0, d1], [out], width(out))
+        return note("v", vec.tensor_tensor_scan, (ap(out), ap(d0), ap(d1), 0.0, MUL, ADD), [d0, d1], [out], width(out))
 
     def cp(out, a):
-        return note(vec.tensor_copy, (ap(out), ap(a)), [a], [out], width(out))
+        return note("v", vec.tensor_copy, (ap(out), ap(a)), [a], [out], width(out))
 
     def fill(name, v, a=0, b=None):
         o = R(name, a, _WORK[name] if b is None else b)
-        return note(vec.memset, (ap(o), v), [], [o], width(o))
+        return note("v", vec.memset, (ap(o), v), [], [o], width(o))
 
     def quant(c, s, src, ext):
-        return note(vec.quantize_mx, (ap(c), ap(s), ap(src)), [], [c, s], 12 + 0.22 * width(src), ext)
+        return note("v", vec.quantize_mx, (ap(c), ap(s), ap(src)), [], [c, s], 12 + 0.22 * width(src), ext)
 
     picks = {}
 
-    def pick(key, dst, src, wid, off, n, ext, tail=0.0):
+    def pick(key, dst, src, wid, off, n, ext, tail=0.0, at=0):
         o = R(off, 0, n)
-        d, w = R(dst + "c", 0, 16 * n), R(src + "c", 0, wid)
-        i = note(vec.tensor_copy, (ap(d).bitcast(dt.uint32), ap(w).bitcast(dt.uint32).indirect(ap(o))), [w, o], [d], 60 + 1.5 * 16 * n, ext, tail)
-        picks[key] = (i, dst, src, wid, off, n, ext)
-        return i
+        c, d, w = 50 + 1.5 * 16 * n, R(dst + "c", at, at + 16 * n), R(src + "c", 0, wid)
+        i = note("v", vec.tensor_copy, (ap(d).bitcast(dt.uint32), ap(w).bitcast(dt.uint32).indirect(ap(o))), [w, o], [d], c, ext, tail)
+        d, w = R(dst + "s", at, at + 16 * n), R(src + "s", 0, wid)
+        j = note("a", sca.activation, (ap(d), ap(w).indirect(ap(o)), COPY), [w, o], [d], c, ext, tail)
+        picks[key] = (i, j)
 
     fill("z32", 0.0)
     fill("gd", 0.0)
     fill("xx", 0.0)
-    fill("kq", 0.0, 256, 272)
-    for n in ("sp0", "sp1", "sp2", "sp3", "out3", "v2"):
+    for h in range(2):
+        fill("kq", 0.0, KH * h + 128, KH * h + KH)
+    for n in ("mk", "da1", "db1", "db3", "v2", "out3"):
         fill(n, 0.0)
     if not mid:
         fill("me2", 0.0)
+        fill("ma3", 0.0)
     fill("base1", float(OWN - PC), 0, 32)
     fill("base1", float(OWN + BLK - PC), 32, 64)
     fill("base3", float(W1 - PC), 0, 32)
     fill("base3", float(W1 + (BLK if mid else 0) - PC), 32, 64)
-    gi = [("gi", 4)]
+    gi = [("gi", 5)]
     P = lambda c: R("pi", c, c + 1)
     F = lambda c: R("pf", c, c + 1)
     ts(P(1), P(0), 15, AND, ext=gi)
@@ -179,60 +188,78 @@ def rank_program(g, core, T, topo):
     ts(F(1), F(0), 16.0, ADD)
     tt(F(5), F(4), F(3), ADD)
     ts(R("k32p", 0, 32), R("z32", 0, 32), F(2), ADD, float(PC), MUL)
+    ts(R("m4", 0, 2), R("z32", 0, 2), F(3), ADD)
+    his = 8 * PC * (1 - e)
+    ts(R("ofh", 0, 16), R("mod16", 0, 16), F(0), ADD, float(his), ADD, ext=gi)
     ts(R("rep", 0, 3), R("z32", 0, 3), F(2), ADD)
     ts(R("rep", 3, 9), R("z32", 0, 6), F(2), ADD, 32.0, ADD)
-    for o in range(2):
-        for t in range(1, RD):
-            half, t1 = (0, t) if t <= 2 else (1, t - 2)
-            ts(R("klist", 4 * o + t - 1, 4 * o + t), F(5), float(64 * (2 * half + o) + LC * (t % 2) + 3 * t1), ADD)
+    for h in range(2):
+        for o in range(2):
+            for t1 in (1, 2):
+                c = 4 * h + 2 * o + t1 - 1
+                ts(R("klist", c, c + 1), F(5), float(64 * o + LC * (t1 % 2) + 3 * t1), ADD)
 
     my = (8 * PC * e, 8 * PC * (e + 1))
     i_w = quant(R("p1c", *my), R("p1s", *my), R("wt", 0, 1024), [("sw", 16)])
     quant(R("p2c", *my), R("p2s", *my), R("wt", 0, 1024), [("sw", 16)])
-    quant(R("xqc", 0, 128 * XA), R("xqs", 0, 128 * XA), R("xt", 0, 512 * XA), [("sxa", 16)])
+    i_xa = quant(R("xqc", 0, 128 * XA), R("xqs", 0, 128 * XA), R("xt", 0, 512 * XA), [("sxa", 16)])
     i_xb = quant(R("xqc", 128 * XA, 128 * RD), R("xqs", 128 * XA, 128 * RD), R("xt", 512 * XA, 512 * RD), [("sxb", 16)])
 
     tt(R("gd", 0, 5 * LC), R("lst", 0, 5 * LC), R("lst", LC, 6 * LC), SUB, [("sdm", 128), ("al", (NR - 1) * n_off)])
     tr(R("xx", 0, 64), R("gd", 0, 64))
     for q in range(4):
-        tr(R("kq", 64 * q, 64 * q + 64), R("xx", 8 * q, 8 * q + 64))
-    E = lambda a, b: R("rec", a, b)
-    O = lambda a, b: R("rec", 64 + a, 64 + b)
+        k = KH * (q // 2) + 64 * (q % 2)
+        tr(R("kq", k, k + 64), R("xx", 8 * q, 8 * q + 64))
+    E = lambda x, a, b: R("rec" + x, a, b)
+    O = lambda x, a, b: R("rec" + x, 32 + a, 32 + b)
+    for h, x in enumerate("ab"):
+        k, l = R("kq", KH * h, KH * h + KH), R("klist", 4 * h, 4 * h + 4)
+        note("v", vec.tensor_copy, (ap(R("rec" + x, 0, 64)), ap(k).indirect(ap(l))), [k, l], [R("rec" + x, 0, 64)], 50 + 1.5 * 64)
 
     def widen(me, b, key):
         return ts(R(me, 32 * b, 32 * b + 32), R("z32", 0, 32), key, LT)
 
-    def steps(t, a, b, first, count, mk):
-        for c in range(count):
-            ts(R("sp%d" % t, a + c, b, 4), R("dr%d" % t, a + c, b, 4), R("mk", mk + c, mk + c + 1), MUL)
+    def widen_a(me, b, m):
+        return af(R(me, 32 * b, 32 * b + 32), R("z32", 0, 32), 1.0, m)
+
+    def M(t, c, n=1):
+        return R("mk", 8 * t + c, 8 * t + c + n)
+
+    def change(x, t, a):
+        d, s = "d%s%d" % (x, t), "s%s%d" % (x, t)
+        ti(R(s, a, 32), M(t, 0, 8), R("m4", 0, (32 - a) // 16), R(d, a, 32), MUL)
+        if t % 2 == 0:
+            tt(E(x, a, 32), E(x, a, 32), R(s, a, 32), ADD)
+            tt(O(x, a, 32), O(x, a, 32), R(s, a, 32), SUB)
+        else:
+            tt(O(x, a, 31), O(x, a, 31), R(s, a, 31), ADD)
+            tt(E(x, a + 1, 32), E(x, a + 1, 32), R(s, a, 31), SUB)
 
     tt(R("dk0", 0, 3), R("kq", 64, 103, 19), R("kq", 0, 39, 19), SUB)
-    note(vec.tensor_copy, (ap(R("rec", 0, 128)), ap(R("kq", 0, 272)).indirect(ap(R("klist", 0, 8)))), [R("kq", 0, 272), R("klist", 0, 8)], [R("rec", 0, 128)], 60 + 1.5 * 128)
-    ts(R("mk", 0, 3), R("dk0", 0, 3), 0.0, GT)
-    tt(R("dr0", 0, 64), O(0, 64), E(0, 64), SUB)
-    steps(0, 0, 64, 0, 3, 0)
-    tt(E(0, 64), E(0, 64), R("sp0", 0, 64), ADD)
-    tt(O(0, 64), O(0, 64), R("sp0", 0, 64), SUB)
-    ts(R("m256", 0, 1), R("dk0", pair, pair + 1), 0.0, GT, 8.0 * PC, MUL)
-    ts(R("me0", 32 * low, 32 * low + 32), R("k32p", 0, 32), R("m256", 0, 1), ADD)
-    ts(R("me0", 32 - 32 * low, 64 - 32 * low), R("k32p", 0, 32), R("m256", 0, 1), SUB, 8.0 * PC, ADD)
+    ts(M(0, 0, 3), R("dk0", 0, 3), 0.0, GT)
+    for x in "ab":
+        tt(R("d%s0" % x, 0, 32), O(x, 0, 32), E(x, 0, 32), SUB)
+        change(x, 0, 0)
+    af(R("m256", 0, 1), M(0, pair), 8.0 * PC, 0.0)
+    af(R("me0", 32 * low, 32 * low + 32), R("k32p", 0, 32), 1.0, R("m256", 0, 1))
+    af(R("m256", 1, 2), R("m256", 0, 1), -1.0, 8.0 * PC)
+    af(R("me0", 32 - 32 * low, 64 - 32 * low), R("k32p", 0, 32), 1.0, R("m256", 1, 2))
     i_v0 = tr(R("v0", 0, 64), R("me0", 0, 64))
-    tt(R("dr1", 0, 63), E(1, 64), O(0, 63), SUB)
+    tt(R("da1", 0, 31), E("a", 1, 32), O("a", 0, 31), SUB)
     for b in range(2):
-        widen("me1", b, R("dr1", 5 * b, 5 * b + 1))
+        widen("me1", b, R("da1", 5 * b, 5 * b + 1))
     tr(R("fm1", 0, 64), R("me1", 0, 64))
-    ts(R("mk", 4, 6), R("dr1", 0, 6, 5), 0.0, GT)
-    steps(1, 16, 63, 0, 2, 4)
-    tt(O(16, 63), O(16, 63), R("sp1", 16, 63), ADD)
-    tt(E(17, 64), E(17, 64), R("sp1", 16, 63), SUB)
+    ts(M(1, 0, 2), R("da1", 0, 6, 5), 0.0, GT)
+    change("a", 1, 16)
+    tt(R("db1", 0, 31), E("b", 1, 32), O("b", 0, 31), SUB)
+    change("b", 1, 0)
 
-    def lanes(i, fm, src, blocks):
+    def lanes(i, fm, blocks):
         inc, ma, eq, pr, sl, off = ["%s%d" % (n, i) for n in ("in", "ma", "eq", "pr", "sl", "off")]
         nn = 48 * len(blocks)
         rc = (0, 6) if len(blocks) == 2 else ((0, 3) if blocks[0] == 0 else (6, 9))
         rep = R("rep", *rc)
         scan(R(inc, 0, 40), R("g40", 0, 40), R(fm, 0, 40))
-        tt(R(ma, 0, 40), R(fm, 0, 40), R(src, 0, 40), MUL)
         ti(R(eq, 0, nn), R(inc, 0, 40), rep, R("n96", 0, nn), EQ)
         ti(R(pr, 0, nn), R(ma, 0, 40), rep, R(eq, 0, nn), MUL)
         scan(R(sl, 0, nn), R("g96", 0, nn), R(pr, 0, nn))
@@ -241,49 +268,54 @@ def rank_program(g, core, T, topo):
         ts(R(off, 1, cols, 2), R(sl, 7, nn, 8), F(1), ADD)
 
     near_blocks = [0, 1] if mid else [near]
-    lanes(1, "fm1", "v0", near_blocks)
+    tt(R("ma1", 0, 40), R("fm1", 0, 40), R("v0", 0, 40), MUL)
+    lanes(1, "fm1", near_blocks)
     aw = [("aw", 2 * n_off)]
     pick("snd1", "snd1", "p1", OWN, "off1", 22 if mid else 10, aw, 9.0)
+    pick("his", "p2", "p1", OWN, "ofh", 16, aw, at=his)
+    tt(R("da2", 0, 16), O("a", 16, 32), E("a", 16, 32), SUB)
+    ts(M(2, 0, 3), R("da2", 0, 11, 5), 0.0, GT)
+    tt(R("db2", 0, 32), O("b", 0, 32), E("b", 0, 32), SUB)
+    change("b", 2, 0)
+    for b, c in ([(0, 0), (1, 2), (2, 1)] if mid else [(near, 1), (2, pair)]):
+        widen_a("me2", b, M(2, c))
+    tr(R("fm2", 0, 96), R("me2", 0, 96))
+    tt(R("db3", 0, 31), E("b", 1, 32), O("b", 0, 31), SUB)
+    for b in range(2):
+        widen("me3", b, R("db3", 5 * b, 5 * b + 1))
+    tr(R("fm3", 0, 64), R("me3", 0, 64))
+    tt(R("e0", 0, 8), blk("v0", 1), blk("v0", 0), SUB)
+    tt(R("f0", 0, 8), R("fm2", 64, 72), R("e0", 0, 8), MUL)
+    for b in near_blocks:
+        tt(blk("out3", b), blk("v0", b), R("f0", 0, 8), SUB if b else ADD)
+    if mid:
+        tt(R("ma3", 0, 40), R("fm3", 0, 40), R("out3", 0, 40), MUL)
+    else:
+        tt(blk("ma3", far), blk("fm3", far), blk("v0", near), MUL)
+        tt(blk("ma3", near), blk("fm3", near), blk("out3", near), MUL)
+    lanes(3, "fm3", [0, 1])
+    pick("snd3", "snd3", "p1", OWN, "off3", 22, aw, 7.5)
+    ts(M(3, 0, 2), R("db3", 0, 6, 5), 0.0, GT)
+    change("b", 3, 16)
     tt(N("bv"), N("base1"), N("v0"), SUB)
-    ts(N("q1"), N("in1"), float(PC), MUL)
+    af(N("q1"), N("in1"), float(PC), 0.0)
     tt(N("q2"), N("q1"), N("bv"), ADD)
     tt(N("q3"), N("fm1"), N("q2"), MUL)
     tt(N("v1"), N("v0"), N("q3"), ADD)
-    tt(R("dr2", 16, 64), O(16, 64), E(16, 64), SUB)
-    for b, c in ([(0, 0), (1, 2), (2, 1)] if mid else [(near, 1), (2, pair)]):
-        widen("me2", b, R("dr2", 16 + 5 * c, 17 + 5 * c))
-    tr(R("fm2", 0, 96), R("me2", 0, 96))
-    ts(R("mk", 8, 11), R("dr2", 16, 27, 5), 0.0, GT)
-    steps(2, 32, 64, 0, 3, 8)
-    tt(E(32, 64), E(32, 64), R("sp2", 32, 64), ADD)
-    tt(O(32, 64), O(32, 64), R("sp2", 32, 64), SUB)
     V1 = [blk("v1" if mid or b == near else "v0", b) for b in range(2)]
     tt(R("e2", 0, 8), V1[1], V1[0], SUB)
     tt(R("f2", 0, 8), R("fm2", 64, 72), R("e2", 0, 8), MUL)
     tt(blk("v2", 0), V1[0], R("f2", 0, 8), ADD)
     tt(blk("v2", 1), V1[1], R("f2", 0, 8), SUB)
-    tt(R("dr3", 32, 63), E(33, 64), O(32, 63), SUB)
-    for b in range(2):
-        widen("me3", b, R("dr3", 32 + 5 * b, 33 + 5 * b))
-    tr(R("fm3", 0, 64), R("me3", 0, 64))
-    if not mid:
-        cp(blk("out3", far), blk("v0", near))
-    ts(N("out3"), N("v2"), float(OWN - PC), MIN)
-    lanes(3, "fm3", "out3", [0, 1])
-    pick("snd3", "snd3", "p1", OWN, "off3", 22, aw, 7.5)
-    ts(R("mk", 12, 14), R("dr3", 32, 38, 5), 0.0, GT)
-    steps(3, 48, 63, 0, 2, 12)
-    tt(O(48, 63), O(48, 63), R("sp3", 48, 63), ADD)
-    tt(E(49, 64), E(49, 64), R("sp3", 48, 63), SUB)
     tt(N("r1"), N("fm1"), N("fm2"), MUL)
     tt(N("ret"), N("fm1"), N("r1"), SUB)
     if mid:
         bf = N("base3")
     else:
         tt(R("far", 0, 8), blk("fm1", far), blk("fm2", near), MUL)
-        ts(N("bf"), R("far", 0, 8), float(BLK), MUL, float(W1 - PC), ADD)
+        af(N("bf"), R("far", 0, 8), float(BLK), float(W1 - PC))
         bf = N("bf")
-    ts(N("nr32"), N("ret"), float(-PC), MUL, float(PC), ADD)
+    af(N("nr32"), N("ret"), float(-PC), float(PC))
     tt(N("g1"), N("v0"), bf, SUB)
     tt(N("g2"), N("ret"), N("g1"), MUL)
     tt(N("g3"), bf, N("v2"), SUB)
@@ -292,133 +324,110 @@ def rank_program(g, core, T, topo):
     tt(N("a2"), N("a1"), N("w4"), ADD)
     tt(N("a3"), N("fm3"), N("a2"), MUL)
     tt(N("v3"), N("v2"), N("a3"), ADD)
-    kc = 48 + 5 * pair
-    tt(R("d4", 0, 1), O(kc, kc + 1), E(kc, kc + 1), SUB)
+    kc = 16 + 5 * pair
+    tt(R("d4", 0, 1), O("b", kc, kc + 1), E("b", kc, kc + 1), SUB)
     widen("me4", 0, R("d4", 0, 1))
     tr(R("fm4", 0, 32), R("me4", 0, 32))
     V3 = [blk("v3" if mid or b == near else "v2", b) for b in range(2)]
     tt(R("e4", 0, 8), V3[1], V3[0], SUB)
     tt(R("f4", 0, 8), R("fm4", 0, 8), R("e4", 0, 8), MUL)
     tt(R("v4", 0, 8), V3[mine], R("f4", 0, 8), ADD if mine == 0 else SUB)
-    where = [blk("v0", mine), V1[mine], blk("v2", mine), V3[mine], R("v4", 0, 8)]
-    n_in1 = sum(2 * (n_off // 2 if s == 1 else n_off) for s in ([0, 2] if mid else [1]))
-    n_in3 = 2 * 2 * (n_off // 2)
-    ext = [aw, [("scp", 32), ("ar1", n_in1)], [("scp", 32), ("ar1", n_in1)], [("ar3", n_in3)], [("ar3", n_in3)]]
-    for t in range(RD):
-        ts(R("of%d" % t, 0, 16, 2), where[t], F(0), ADD)
-        ts(R("of%d" % t, 1, 16, 2), where[t], F(1), ADD)
-        pick(t, "st%d" % t, "p1" if t == 0 else "p2", (OWN, W1, W1, W3, W3)[t], "of%d" % t, 16, ext[t], 2.5)
 
     def out_of(t, h):
         bank, c = 512 * ((2 * t + h) % 8), 256 * t + 128 * h
         return T.yb[:, c:c + 128], T.ps[:, bank:bank + 128]
-    i_ev = {}
-    for t in (3, 4):
-        i_ev[t] = note(vec.tensor_copy, out_of(t, 0), [R("st%dc" % t, 0, 1)], [R("yb", 256 * t, 256 * t + 128)], 128, [("mm", 2 * t + 1)], 2.0)
+
+    where = [blk("v0", mine), V1[mine], blk("v2", mine), V3[mine], R("v4", 0, 8)]
+    n_in1 = sum(2 * (n_off // 2 if s == 1 else n_off) for s in ([0, 2] if mid else [1]))
+    n_in3 = 2 * 2 * (n_off // 2)
+    ext = [aw, [("ar1", n_in1)], [("ar1", n_in1)], [("ar3", n_in3)], [("ar3", n_in3)]]
+    evac, later = {}, []
+    for t in range(RD):
+        later.append(ts(R("of%d" % t, 0, 16, 2), where[t], F(0), ADD))
+        later.append(ts(R("of%d" % t, 1, 16, 2), where[t], F(1), ADD))
+        pick(t, "st%d" % t, "p1" if t == 0 else "p2", (OWN, W1, W1, W3, W3)[t], "of%d" % t, 16, ext[t], 2.5 if t == 4 else 0.0)
+        for h in range(2):
+            q = "v" if t >= 3 and h == 0 else "a"
+            args = out_of(t, h) if q == "v" else out_of(t, h) + (COPY,)
+            evac[t, h] = note(q, vec.tensor_copy if q == "v" else sca.activation, args,
+                              [R("st%dc" % t, 0, 1), R("st%ds" % t, 0, 1), R("xqc", 0, 128 * t + 128)],
+                              [R("yb", 256 * t + 128 * h, 256 * t + 128 * h + 128)], 128, [("mm", 2 * t + h + 1)], 2.0 if t == 4 else 1.0, T_PE)
 
     n_ops = len(ops)
+    queue = [o[0] for o in ops]
     raw = [set() for _ in ops]
     seq = [set() for _ in ops]
     hist = {}
-    for i, (call, args, reads, writes, ex, cost, tail) in enumerate(ops):
-        for kind, regs in (("r", reads), ("w", writes)):
+    for i, o in enumerate(ops):
+        for kind, regs in (("r", o[4]), ("w", o[5])):
             for name, a, b, step in regs:
                 cols = set(range(a, b, step))
                 for j, k2, c2 in hist.get(name, []):
                     if j != i and (kind == "w" or k2 == "w") and not cols.isdisjoint(c2):
-                        (raw if k2 == "w" else seq)[i].add(j)
-        for kind, regs in (("r", reads), ("w", writes)):
+                        (raw if k2 == "w" or queue[j] != queue[i] else seq)[i].add(j)
+        for kind, regs in (("r", o[4]), ("w", o[5])):
             for name, a, b, step in regs:
                 hist.setdefault(name, []).append((i, kind, set(range(a, b, step))))
+    for a, b in (("snd1", "snd3"), ("snd3", 0), ("snd3", "his"), (0, 1), (1, 2), (2, 3), (3, 4)):
+        for n in range(2):
+            seq[picks[b][n]].add(picks[a][n])
+    for i in [i_xb] + later:
+        seq[i].add(picks["snd3"][0])
     prio = [0.0] * n_ops
     for i in range(n_ops - 1, -1, -1):
-        prio[i] += ops[i][5] + ops[i][6]
+        prio[i] += ops[i][7] + ops[i][8]
         for j in raw[i]:
             prio[j] = max(prio[j], prio[i] + T_WAKE)
         for j in seq[i]:
             prio[j] = max(prio[j], prio[i])
-    done, tok, now = {}, {}, 0.0
-    while len(tok) < n_ops:
+    done, tok, now, count, order = {}, {}, {"v": 0.0, "a": 0.6}, {"v": 0, "a": 0}, []
+    while len(order) < n_ops:
         best = None
         for i in range(n_ops):
             if i in tok or not all(j in tok for j in raw[i]) or not all(j in tok for j in seq[i]):
                 continue
-            at = max([now] + [done[j] + T_WAKE for j in raw[i]] + [T_EXT.get(s, 0.0) for s, _ in ops[i][4]])
+            at = max([now[queue[i]]] + [done[j] + T_WAKE + ops[i][9] for j in raw[i]] + [T_EXT.get(s, 0.0) for s, _ in ops[i][6]])
             if best is None or (at, -prio[i]) < best[:2]:
                 best = (at, -prio[i], i)
         i = best[2]
-        now = done[i] = best[0] + ops[i][5]
-        tok[i] = len(tok) + 1
-    waited = {}
-
-    def vwait(sem, n):
-        if waited.get(sem, 0) < n:
-            vec.wait_ge(S[sem], n)
-            waited[sem] = n
-
-    for i in sorted(range(n_ops), key=lambda k: tok[k]):
-        call, args, reads, writes, ex, cost, tail = ops[i]
-        for sem, n in ex:
-            vwait(sem, n)
-        vwait("v", max([0] + [tok[j] for j in raw[i]]))
-        call(*args).then_inc(S.v, 1)
+        q = queue[i]
+        now[q] = done[i] = best[0] + ops[i][7]
+        count[q] += 1
+        tok[i] = count[q]
+        order.append(i)
 
     for b in range(4):
-        for h, q in ((0, g.sync), (1, g.scalar)):
+        for h, q in ((0, g.sync), (1, sca)):
             p0 = 32 * b + 16 * h
             q.dma_start(T.lst[p0:p0 + 16, LC * r:LC * r + LC], T.dm[:, 6 * h:6 * h + LC]).then_inc(S.sdm, 16)
     g.sync.dma_start(T.wt[:], T.w[:]).then_inc(S.sw, 16)
     g.sync.dma_start(T.xt[:, 0:512 * XA], T.x[:, 0:512 * XA]).then_inc(S.sxa, 16)
     g.sync.wait_ge(S.v, tok[i_v0])
     g.sync.dma_start(T.xt[:, 512 * XA:], T.x[:, 512 * XA:]).then_inc(S.sxb, 16)
-    his = slice(8 * PC * (1 - e), 8 * PC * (2 - e))
-    g.sync.wait_ge(S.aw, 2 * n_off)
-    g.sync.dma_start(T.p2c[:, his].bitcast(dt.uint8), T.p1c[:, his].bitcast(dt.uint8)).then_inc(S.scp, 16)
-    g.sync.dma_start(T.p2s[:, his], T.p1s[:, his]).then_inc(S.scp, 16)
 
-    acount, asem, swaited = [0], {}, {}
+    waited = {}
 
-    def swait(sem, n):
-        if swaited.get(sem, 0) < n:
-            g.scalar.wait_ge(S[sem], n)
-            swaited[sem] = n
+    def wait(q, sem, n):
+        if waited.get((q, sem), 0) < n:
+            (vec if q == "v" else sca).wait_ge(S[sem], n)
+            waited[q, sem] = n
 
-    def scales(key):
-        i, dst, src, wid, off, n, ex = picks[key]
-        for sem, c in ex:
-            swait(sem, c)
-        swait("v", max([0] + [tok[j] for j in raw[i]]))
-        g.scalar.activation(T[dst + "s"][:, 0:16 * n], T[src + "s"][:, 0:wid].indirect(T[off][:, 0:n]), COPY).then_inc(S.a, 1)
-        acount[0] += 1
-        asem[key] = acount[0]
-
-    def evac(t, h):
-        swait("mm", 2 * t + h + 1)
-        g.scalar.activation(*out_of(t, h), COPY).then_inc(S.a, 1)
-        acount[0] += 1
-        asem["y%d" % t] = acount[0]
-
-    for key in sorted(("snd1", "snd3", 0), key=lambda k: tok[picks[k][0]]):
-        scales(key)
-    evac(0, 0)
-    evac(0, 1)
-    scales(1)
-    scales(2)
-    for t in (1, 2):
-        evac(t, 0)
-        evac(t, 1)
-    scales(3)
-    scales(4)
-    evac(3, 1)
-    evac(4, 1)
+    for i in order:
+        q, call, args, kw, reads, writes, ex, cost, tail, lag = ops[i]
+        for sem, n in ex:
+            wait(q, sem, n)
+        for s in ("v", "a"):
+            wait(q, s, max([0] + [tok[j] for j in raw[i] if queue[j] == s]))
+        call(*args, **kw).then_inc(S[q], 1)
 
     big = {"allow_small_or_imprecise_dtypes": True}
     g.iota(T.pi[:, 0:1], [[0, 1]], 0, 1).then_inc(S.gi, 1)
     g.iota(T.mod32[:], [[0, 2], [1, 32]], 0, 0, **big).then_inc(S.gi, 1)
     g.iota(T.mod8[:], [[0, 12], [1, 8]], 0, 0, **big).then_inc(S.gi, 1)
     g.iota(T.n96[:], [[0, 2], [1, 6], [0, 8]], 1, 0, **big).then_inc(S.gi, 1)
+    g.iota(T.mod16[:], [[16, 16]], 0, 0, **big).then_inc(S.gi, 1)
     left = [0]
-    others = [q for q in range(NR) if q != r]
+    others = sorted([q for q in range(NR) if q != r], key=lambda q: (q // 2 != 1, (q - r) % NR))
     mycol = T.lst[:, LC * r:LC * r + LC]
     g.wait_ge(S.sdm, 128)
     g.remote_dma_fused([RemoteDMATransfer(
@@ -440,7 +449,7 @@ def rank_program(g, core, T, topo):
         per = len(eng) // len(jobs)
         for kind in ("c", "s"):
             if kind == "s":
-                g.wait_ge(S.a, asem[key])
+                g.wait_ge(S.a, tok[picks[key][1]])
             trs = []
             for n, (a, q, p) in enumerate(jobs):
                 src, dst = T[key + kind][:, a:a + BLK], T["p2" + kind][:, p:p + BLK]
@@ -470,17 +479,20 @@ def rank_program(g, core, T, topo):
     send(3, jobs)
 
     for t in range(RD):
-        g.tensor.wait_ge(S.v, max([tok[picks[t][0]], tok[i_xb if t >= XA else i_xb - 1]]))
-        g.tensor.wait_ge(S.a, asem[t])
+        g.tensor.wait_ge(S.v, max(tok[picks[t][0]], tok[i_xa if t < XA else i_xb]))
+        g.tensor.wait_ge(S.a, tok[picks[t][1]])
         for h in range(2):
+            if t == 4:
+                g.tensor.wait_ge(S.a, tok[evac[0, h]])
             st, c = slice(128 * h, 128 * h + 128), slice(128 * t, 128 * t + 128)
             g.tensor.matmul_mx(out_of(t, h)[1], T["st%dc" % t][:, st], T["st%ds" % t][:, st], T.xqc[:, c], T.xqs[:, c], True, True).then_inc(S.mm, 1)
 
     for t in range(RD):
-        if t in i_ev:
-            g.sync.wait_ge(S.v, tok[i_ev[t]])
-        g.sync.wait_ge(S.a, asem["y%d" % t])
+        for h in range(2):
+            i = evac[t, h]
+            g.sync.wait_ge(S[queue[i]], tok[i])
         g.sync.dma_start(T.y[:, 256 * t:256 * t + 256], T.yb[:, 256 * t:256 * t + 256]).then_inc(S.sy, 16)
-    g.sync.wait_ge(S.v, n_ops)
+    g.sync.wait_ge(S.v, count["v"])
+    g.sync.wait_ge(S.a, count["a"])
     g.sync.wait_ge(S.sy, 16 * RD)
     g.wait_ge(S.loc, left[0])

from concourse.bass import DstId, RemoteDMATransfer
from concourse.mybir import dt, AluOpType, ActivationFunctionType

NR = 6
RD = 5
PC = 32
LANES = 5
BLK = LANES * PC
OWN = 16 * PC
W1 = OWN + 2 * BLK
W3 = W1 + 2 * BLK
LC = 9
SB = 12 * PC - PC
XA = 3
KH = 144

F32 = "float32"
SCRATCH = {
    "wt": ("sbuf", [128, 1024], "bfloat16"),
    "xt": ("sbuf", [128, 512 * RD], "bfloat16"),
    "lst": ("sbuf", [128, 56], "int32"),
    "p1c": ("sbuf", [128, OWN], "float8_e4m3fn_x4"), "p1s": ("sbuf", [128, OWN], "uint8"),
    "p2c": ("sbuf", [128, W3], "float8_e4m3fn_x4"), "p2s": ("sbuf", [128, W3], "uint8"),
    "snd1c": ("sbuf", [128, SB], "float8_e4m3fn_x4"), "snd1s": ("sbuf", [128, SB], "uint8"),
    "snd3c": ("sbuf", [128, SB], "float8_e4m3fn_x4"), "snd3s": ("sbuf", [128, SB], "uint8"),
    "xqc": ("sbuf", [128, 128 * RD], "float8_e4m3fn_x4"), "xqs": ("sbuf", [128, 128 * RD], "uint8"),
    "yb": ("sbuf", [128, 256 * RD], F32),
    "ps": ("psum", [128, 4096], F32),
    "pi": ("sbuf", [128, 8], "int32"),
    "klist": ("sbuf", [128, 8], "uint16"), "rep": ("sbuf", [128, 12], "uint16"), "m4": ("sbuf", [128, 2], "uint16"),
    "off1": ("sbuf", [128, 24], "uint16"), "off3": ("sbuf", [128, 24], "uint16"), "ofh": ("sbuf", [128, 16], "uint16"),
}
for _t in range(RD):
    SCRATCH["of%d" % _t] = ("sbuf", [128, 16], "uint16")
    SCRATCH["st%dc" % _t] = ("sbuf", [128, 256], "float8_e4m3fn_x4")
    SCRATCH["st%ds" % _t] = ("sbuf", [128, 256], "uint8")
_WORK = {
    "pf": 8, "z32": 32, "k32p": 32, "mod16": 16, "mod32": 64, "g40": 64, "mod8": 96, "g96": 96, "n96": 96, "base1": 64, "base3": 64,
    "gd": 64, "xx": 96, "kq": 2 * KH, "reca": 64, "recb": 64, "dk0": 4, "d4": 4, "mk": 32, "m256": 4,
    "da0": 32, "db0": 32, "da1": 32, "db1": 32, "da2": 16, "db2": 32, "db3": 32,
    "sa0": 32, "sb0": 32, "sa1": 32, "sb1": 32, "sb2": 32, "sb3": 32,
    "me0": 64, "me1": 64, "me2": 96, "me3": 64, "me4": 32,
    "v0": 64, "fm1": 64, "fm2": 96, "fm3": 64, "fm4": 32, "v1": 64, "v2": 64, "v3": 64, "v4": 8,
    "in1": 64, "ma1": 64, "eq1": 96, "pr1": 96, "sl1": 96, "in3": 64, "ma3": 64, "eq3": 96, "pr3": 96, "sl3": 96,
    "out3": 64, "e0": 8, "f0": 8, "bv": 64, "q1": 64, "q2": 64, "q3": 64, "e2": 8, "f2": 8, "r1": 64, "ret": 64, "far": 8,
    "bf": 64, "nr32": 64, "g1": 64, "g2": 64, "g3": 64, "w4": 64, "a1": 64, "a2": 64, "a3": 64, "e4": 8, "f4": 8,
}
for _n in _WORK:
    SCRATCH[_n] = ("sbuf", [128, _WORK[_n]], F32)

SEMAPHORES = ["v", "a", "mm", "gi", "sdm", "sw", "sxa", "sxb", "sy", "al", "aw", "ar1", "ar3", "loc"]

ADD, SUB, MUL, MIN = AluOpType.add, AluOpType.subtract, AluOpType.mult, AluOpType.min
LT, GT, EQ = AluOpType.is_lt, AluOpType.is_gt, AluOpType.is_equal
AND, SHR = AluOpType.bitwise_and, AluOpType.logical_shift_right
COPY, IDENT = ActivationFunctionType.Copy, ActivationFunctionType.Identity

T_WAKE, T_CYC, T_PE = 0.1, 0.001, 0.3
T_EXT = {"gi": 1.2, "sw": 3.4, "sxa": 5.0, "al": 6.0, "aw": 8.5, "sxb": 10.5, "ar1": 13.5, "ar3": 17.0}


def R(name, a, b, step=1):
    return (name, a, b, step)


def rank_program(g, core, T, topo):
    r = T.rank_of(core)
    if r is None:
        return
    cores = T.cores
    pair = r // 2
    base, e = 2 * pair, r % 2
    mate = base + 1 - e
    mid = pair == 1
    vec, sca = g.vector, g.scalar
    S = T.sem

    near = None if mid else (0 if pair == 0 else 1)
    far = None if mid else 1 - near
    nb = (0, 40) if mid else (32 * near, 32 * near + 8)
    low = 0 if mid else 1
    mine = low if e == 0 else 1 - low

    def N(name):
        return R(name, nb[0], nb[1])

    def blk(name, b):
        return R(name, 32 * b, 32 * b + 8)

    def ap(o):
        name, a, b, step = o
        return T[name][:, a:b] if step == 1 else T[name][:, a:b:step]

    def sender(s, q):
        for m in (2 * s, 2 * s + 1):
            if topo.same_plane(topo.chip(cores[m]), topo.chip(cores[q])):
                return m
        return 2 * s

    def peers(s):
        return [q for q in (2 * s, 2 * s + 1) if sender(pair, q) == r]

    n_off = len(topo.engines(core, cores[mate]))

    def addr(q):
        rid, pid, _ = topo.addr(cores[q])
        return rid, pid

    ops = []

    def note(q, call, args, reads, writes, cost, ext=(), tail=0.0, lag=0.0, kw=None):
        ops.append((q, call, args, kw or {}, reads, writes, tuple(ext), max(64, cost) * T_CYC, tail, lag))
        return len(ops) - 1

    def val(x):
        return ap(x) if isinstance(x, tuple) else x

    def width(o):
        return len(range(o[1], o[2], o[3]))

    def ts(out, in0, s1, op0, s2=None, op1=None, ext=()):
        args = (ap(out), ap(in0), val(s1), None, op0) if op1 is None else (ap(out), ap(in0), val(s1), val(s2), op0, op1)
        return note("v", vec.tensor_scalar, args, [x for x in (in0, s1, s2) if isinstance(x, tuple)], [out], width(out), ext)

    def af(out, in0, scale, bias):
        return note("a", sca.activation, (ap(out), ap(in0), IDENT), [x for x in (in0, scale, bias) if isinstance(x, tuple)], [out],
                    width(out), kw={"bias": val(bias), "scale": val(scale)})

    def tt(out, a, b, op, ext=()):
        return note("v", vec.tensor_tensor, (ap(out), ap(a), ap(b), op), [a, b], [out], 2 * width(out), ext)

    def ti(out, win, off, b, op):
        return note("v", vec.tensor_tensor, (ap(out), ap(win).indirect(ap(off)), ap(b), op), [win, off, b], [out], 50 + 1.5 * width(out))

    def tr(out, a):
        return note("v", vec.transpose, (ap(out), ap(a)), [a], [out], width(out))

    def scan(out, d0, d1):
        return note("v", vec.tensor_tensor_scan, (ap(out), ap(d0), ap(d1), 0.0, MUL, ADD), [d0, d1], [out], width(out))

    def cp(out, a):
        return note("v", vec.tensor_copy, (ap(out), ap(a)), [a], [out], width(out))

    def fill(name, v, a=0, b=None):
        o = R(name, a, _WORK[name] if b is None else b)
        return note("v", vec.memset, (ap(o), v), [], [o], width(o))

    def quant(c, s, src, ext):
        return note("v", vec.quantize_mx, (ap(c), ap(s), ap(src)), [], [c, s], 12 + 0.22 * width(src), ext)

    picks = {}

    def pick(key, dst, src, wid, off, n, ext, tail=0.0, at=0):
        o = R(off, 0, n)
        c, d, w = 50 + 1.5 * 16 * n, R(dst + "c", at, at + 16 * n), R(src + "c", 0, wid)
        i = note("v", vec.tensor_copy, (ap(d).bitcast(dt.uint32), ap(w).bitcast(dt.uint32).indirect(ap(o))), [w, o], [d], c, ext, tail)
        d, w = R(dst + "s", at, at + 16 * n), R(src + "s", 0, wid)
        j = note("a", sca.activation, (ap(d), ap(w).indirect(ap(o)), COPY), [w, o], [d], c, ext, tail)
        picks[key] = (i, j)

    fill("z32", 0.0)
    fill("gd", 0.0)
    fill("xx", 0.0)
    for h in range(2):
        fill("kq", 0.0, KH * h + 128, KH * h + KH)
    for n in ("mk", "da1", "db1", "db3", "v2", "out3"):
        fill(n, 0.0)
    if not mid:
        fill("me2", 0.0)
        fill("ma3", 0.0)
    fill("base1", float(OWN - PC), 0, 32)
    fill("base1", float(OWN + BLK - PC), 32, 64)
    fill("base3", float(W1 - PC), 0, 32)
    fill("base3", float(W1 + (BLK if mid else 0) - PC), 32, 64)
    gi = [("gi", 5)]
    P = lambda c: R("pi", c, c + 1)
    F = lambda c: R("pf", c, c + 1)
    ts(P(1), P(0), 15, AND, ext=gi)
    ts(P(2), P(0), 7, AND, ext=gi)
    ts(P(3), P(0), 3, AND, ext=gi)
    ts(P(4), P(0), 2, SHR, 3, AND, ext=gi)
    ts(R("g40", 0, 64), R("mod32", 0, 64), 1.0, MIN, ext=gi)
    ts(R("g96", 0, 96), R("mod8", 0, 96), 1.0, MIN, ext=gi)
    cp(F(0), P(1))
    cp(F(2), P(2))
    cp(F(3), P(3))
    ts(F(4), P(4), 18.0, MUL)
    ts(F(1), F(0), 16.0, ADD)
    tt(F(5), F(4), F(3), ADD)
    ts(R("k32p", 0, 32), R("z32", 0, 32), F(2), ADD, float(PC), MUL)
    ts(R("m4", 0, 2), R("z32", 0, 2), F(3), ADD)
    his = 8 * PC * (1 - e)
    ts(R("ofh", 0, 16), R("mod16", 0, 16), F(0), ADD, float(his), ADD, ext=gi)
    ts(R("rep", 0, 3), R("z32", 0, 3), F(2), ADD)
    ts(R("rep", 3, 9), R("z32", 0, 6), F(2), ADD, 32.0, ADD)
    for h in range(2):
        for o in range(2):
            for t1 in (1, 2):
                c = 4 * h + 2 * o + t1 - 1
                ts(R("klist", c, c + 1), F(5), float(64 * o + LC * (t1 % 2) + 3 * t1), ADD)

    my = (8 * PC * e, 8 * PC * (e + 1))
    i_w = quant(R("p1c", *my), R("p1s", *my), R("wt", 0, 1024), [("sw", 16)])
    quant(R("p2c", *my), R("p2s", *my), R("wt", 0, 1024), [("sw", 16)])
    i_xa = quant(R("xqc", 0, 128 * XA), R("xqs", 0, 128 * XA), R("xt", 0, 512 * XA), [("sxa", 16)])
    i_xb = quant(R("xqc", 128 * XA, 128 * RD), R("xqs", 128 * XA, 128 * RD), R("xt", 512 * XA, 512 * RD), [("sxb", 16)])

    tt(R("gd", 0, 5 * LC), R("lst", 0, 5 * LC), R("lst", LC, 6 * LC), SUB, [("sdm", 128), ("al", (NR - 1) * n_off)])
    tr(R("xx", 0, 64), R("gd", 0, 64))
    for q in range(4):
        k = KH * (q // 2) + 64 * (q % 2)
        tr(R("kq", k, k + 64), R("xx", 8 * q, 8 * q + 64))
    E = lambda x, a, b: R("rec" + x, a, b)
    O = lambda x, a, b: R("rec" + x, 32 + a, 32 + b)
    for h, x in enumerate("ab"):
        k, l = R("kq", KH * h, KH * h + KH), R("klist", 4 * h, 4 * h + 4)
        note("v", vec.tensor_copy, (ap(R("rec" + x, 0, 64)), ap(k).indirect(ap(l))), [k, l], [R("rec" + x, 0, 64)], 50 + 1.5 * 64)

    def widen(me, b, key):
        return ts(R(me, 32 * b, 32 * b + 32), R("z32", 0, 32), key, LT)

    def widen_a(me, b, m):
        return af(R(me, 32 * b, 32 * b + 32), R("z32", 0, 32), 1.0, m)

    def M(t, c, n=1):
        return R("mk", 8 * t + c, 8 * t + c + n)

    def change(x, t, a):
        d, s = "d%s%d" % (x, t), "s%s%d" % (x, t)
        ti(R(s, a, 32), M(t, 0, 8), R("m4", 0, (32 - a) // 16), R(d, a, 32), MUL)
        if t % 2 == 0:
            tt(E(x, a, 32), E(x, a, 32), R(s, a, 32), ADD)
            tt(O(x, a, 32), O(x, a, 32), R(s, a, 32), SUB)
        else:
            tt(O(x, a, 31), O(x, a, 31), R(s, a, 31), ADD)
            tt(E(x, a + 1, 32), E(x, a + 1, 32), R(s, a, 31), SUB)

    tt(R("dk0", 0, 3), R("kq", 64, 103, 19), R("kq", 0, 39, 19), SUB)
    ts(M(0, 0, 3), R("dk0", 0, 3), 0.0, GT)
    for x in "ab":
        tt(R("d%s0" % x, 0, 32), O(x, 0, 32), E(x, 0, 32), SUB)
        change(x, 0, 0)
    af(R("m256", 0, 1), M(0, pair), 8.0 * PC, 0.0)
    af(R("me0", 32 * low, 32 * low + 32), R("k32p", 0, 32), 1.0, R("m256", 0, 1))
    af(R("m256", 1, 2), R("m256", 0, 1), -1.0, 8.0 * PC)
    af(R("me0", 32 - 32 * low, 64 - 32 * low), R("k32p", 0, 32), 1.0, R("m256", 1, 2))
    i_v0 = tr(R("v0", 0, 64), R("me0", 0, 64))
    tt(R("da1", 0, 31), E("a", 1, 32), O("a", 0, 31), SUB)
    for b in range(2):
        widen("me1", b, R("da1", 5 * b, 5 * b + 1))
    tr(R("fm1", 0, 64), R("me1", 0, 64))
    ts(M(1, 0, 2), R("da1", 0, 6, 5), 0.0, GT)
    change("a", 1, 16)
    tt(R("db1", 0, 31), E("b", 1, 32), O("b", 0, 31), SUB)
    change("b", 1, 0)

    def lanes(i, fm, blocks):
        inc, ma, eq, pr, sl, off = ["%s%d" % (n, i) for n in ("in", "ma", "eq", "pr", "sl", "off")]
        nn = 48 * len(blocks)
        rc = (0, 6) if len(blocks) == 2 else ((0, 3) if blocks[0] == 0 else (6, 9))
        rep = R("rep", *rc)
        scan(R(inc, 0, 40), R("g40", 0, 40), R(fm, 0, 40))
        ti(R(eq, 0, nn), R(inc, 0, 40), rep, R("n96", 0, nn), EQ)
        ti(R(pr, 0, nn), R(ma, 0, 40), rep, R(eq, 0, nn), MUL)
        scan(R(sl, 0, nn), R("g96", 0, nn), R(pr, 0, nn))
        cols = 12 * len(blocks)
        ts(R(off, 0, cols, 2), R(sl, 7, nn, 8), F(0), ADD)
        ts(R(off, 1, cols, 2), R(sl, 7, nn, 8), F(1), ADD)

    near_blocks = [0, 1] if mid else [near]
    tt(R("ma1", 0, 40), R("fm1", 0, 40), R("v0", 0, 40), MUL)
    lanes(1, "fm1", near_blocks)
    aw = [("aw", 2 * n_off)]
    pick("snd1", "snd1", "p1", OWN, "off1", 22 if mid else 10, aw, 9.0)
    pick("his", "p2", "p1", OWN, "ofh", 16, aw, at=his)
    tt(R("da2", 0, 16), O("a", 16, 32), E("a", 16, 32), SUB)
    ts(M(2, 0, 3), R("da2", 0, 11, 5), 0.0, GT)
    tt(R("db2", 0, 32), O("b", 0, 32), E("b", 0, 32), SUB)
    change("b", 2, 0)
    for b, c in ([(0, 0), (1, 2), (2, 1)] if mid else [(near, 1), (2, pair)]):
        widen_a("me2", b, M(2, c))
    tr(R("fm2", 0, 96), R("me2", 0, 96))
    tt(R("db3", 0, 31), E("b", 1, 32), O("b", 0, 31), SUB)
    for b in range(2):
        widen("me3", b, R("db3", 5 * b, 5 * b + 1))
    tr(R("fm3", 0, 64), R("me3", 0, 64))
    tt(R("e0", 0, 8), blk("v0", 1), blk("v0", 0), SUB)
    tt(R("f0", 0, 8), R("fm2", 64, 72), R("e0", 0, 8), MUL)
    for b in near_blocks:
        tt(blk("out3", b), blk("v0", b), R("f0", 0, 8), SUB if b else ADD)
    if mid:
        tt(R("ma3", 0, 40), R("fm3", 0, 40), R("out3", 0, 40), MUL)
    else:
        tt(blk("ma3", far), blk("fm3", far), blk("v0", near), MUL)
        tt(blk("ma3", near), blk("fm3", near), blk("out3", near), MUL)
    lanes(3, "fm3", [0, 1])
    pick("snd3", "snd3", "p1", OWN, "off3", 22, aw, 7.5)
    ts(M(3, 0, 2), R("db3", 0, 6, 5), 0.0, GT)
    change("b", 3, 16)
    tt(N("bv"), N("base1"), N("v0"), SUB)
    af(N("q1"), N("in1"), float(PC), 0.0)
    tt(N("q2"), N("q1"), N("bv"), ADD)
    tt(N("q3"), N("fm1"), N("q2"), MUL)
    tt(N("v1"), N("v0"), N("q3"), ADD)
    V1 = [blk("v1" if mid or b == near else "v0", b) for b in range(2)]
    tt(R("e2", 0, 8), V1[1], V1[0], SUB)
    tt(R("f2", 0, 8), R("fm2", 64, 72), R("e2", 0, 8), MUL)
    tt(blk("v2", 0), V1[0], R("f2", 0, 8), ADD)
    tt(blk("v2", 1), V1[1], R("f2", 0, 8), SUB)
    tt(N("r1"), N("fm1"), N("fm2"), MUL)
    tt(N("ret"), N("fm1"), N("r1"), SUB)
    if mid:
        bf = N("base3")
    else:
        tt(R("far", 0, 8), blk("fm1", far), blk("fm2", near), MUL)
        af(N("bf"), R("far", 0, 8), float(BLK), float(W1 - PC))
        bf = N("bf")
    af(N("nr32"), N("ret"), float(-PC), float(PC))
    tt(N("g1"), N("v0"), bf, SUB)
    tt(N("g2"), N("ret"), N("g1"), MUL)
    tt(N("g3"), bf, N("v2"), SUB)
    tt(N("w4"), N("g2"), N("g3"), ADD)
    tt(N("a1"), N("nr32"), N("in3"), MUL)
    tt(N("a2"), N("a1"), N("w4"), ADD)
    tt(N("a3"), N("fm3"), N("a2"), MUL)
    tt(N("v3"), N("v2"), N("a3"), ADD)
    kc = 16 + 5 * pair
    tt(R("d4", 0, 1), O("b", kc, kc + 1), E("b", kc, kc + 1), SUB)
    widen("me4", 0, R("d4", 0, 1))
    tr(R("fm4", 0, 32), R("me4", 0, 32))
    V3 = [blk("v3" if mid or b == near else "v2", b) for b in range(2)]
    tt(R("e4", 0, 8), V3[1], V3[0], SUB)
    tt(R("f4", 0, 8), R("fm4", 0, 8), R("e4", 0, 8), MUL)
    tt(R("v4", 0, 8), V3[mine], R("f4", 0, 8), ADD if mine == 0 else SUB)

    def out_of(t, h):
        bank, c = 512 * ((2 * t + h) % 8), 256 * t + 128 * h
        return T.yb[:, c:c + 128], T.ps[:, bank:bank + 128]

    where = [blk("v0", mine), V1[mine], blk("v2", mine), V3[mine], R("v4", 0, 8)]
    n_in1 = sum(2 * (n_off // 2 if s == 1 else n_off) for s in ([0, 2] if mid else [1]))
    n_in3 = 2 * 2 * (n_off // 2)
    ext = [aw, [("ar1", n_in1)], [("ar1", n_in1)], [("ar3", n_in3)], [("ar3", n_in3)]]
    evac, later = {}, []
    for t in range(RD):
        later.append(ts(R("of%d" % t, 0, 16, 2), where[t], F(0), ADD))
        later.append(ts(R("of%d" % t, 1, 16, 2), where[t], F(1), ADD))
        pick(t, "st%d" % t, "p1" if t == 0 else "p2", (OWN, W1, W1, W3, W3)[t], "of%d" % t, 16, ext[t], 2.5 if t == 4 else 0.0)
        for h in range(2):
            q = "v" if t >= 3 and h == 0 else "a"
            args = out_of(t, h) if q == "v" else out_of(t, h) + (COPY,)
            evac[t, h] = note(q, vec.tensor_copy if q == "v" else sca.activation, args,
                              [R("st%dc" % t, 0, 1), R("st%ds" % t, 0, 1), R("xqc", 0, 128 * t + 128)],
                              [R("yb", 256 * t + 128 * h, 256 * t + 128 * h + 128)], 128, [("mm", 2 * t + h + 1)], 2.0 if t == 4 else 1.0, T_PE)

    n_ops = len(ops)
    queue = [o[0] for o in ops]
    raw = [set() for _ in ops]
    seq = [set() for _ in ops]
    hist = {}
    for i, o in enumerate(ops):
        for kind, regs in (("r", o[4]), ("w", o[5])):
            for name, a, b, step in regs:
                cols = set(range(a, b, step))
                for j, k2, c2 in hist.get(name, []):
                    if j != i and (kind == "w" or k2 == "w") and not cols.isdisjoint(c2):
                        (raw if k2 == "w" or queue[j] != queue[i] else seq)[i].add(j)
        for kind, regs in (("r", o[4]), ("w", o[5])):
            for name, a, b, step in regs:
                hist.setdefault(name, []).append((i, kind, set(range(a, b, step))))
    for a, b in (("snd1", "snd3"), ("snd3", 0), ("snd3", "his"), (0, 1), (1, 2), (2, 3), (3, 4)):
        for n in range(2):
            seq[picks[b][n]].add(picks[a][n])
    for i in [i_xb] + later:
        seq[i].add(picks["snd3"][0])
    prio = [0.0] * n_ops
    for i in range(n_ops - 1, -1, -1):
        prio[i] += ops[i][7] + ops[i][8]
        for j in raw[i]:
            prio[j] = max(prio[j], prio[i] + T_WAKE)
        for j in seq[i]:
            prio[j] = max(prio[j], prio[i])
    done, tok, now, count, order = {}, {}, {"v": 0.0, "a": 0.6}, {"v": 0, "a": 0}, []
    while len(order) < n_ops:
        best = None
        for i in range(n_ops):
            if i in tok or not all(j in tok for j in raw[i]) or not all(j in tok for j in seq[i]):
                continue
            at = max([now[queue[i]]] + [done[j] + T_WAKE + ops[i][9] for j in raw[i]] + [T_EXT.get(s, 0.0) for s, _ in ops[i][6]])
            if best is None or (at, -prio[i]) < best[:2]:
                best = (at, -prio[i], i)
        i = best[2]
        q = queue[i]
        now[q] = done[i] = best[0] + ops[i][7]
        count[q] += 1
        tok[i] = count[q]
        order.append(i)

    for b in range(4):
        for h, q in ((0, g.sync), (1, sca)):
            p0 = 32 * b + 16 * h
            q.dma_start(T.lst[p0:p0 + 16, LC * r:LC * r + LC], T.dm[:, 6 * h:6 * h + LC]).then_inc(S.sdm, 16)
    g.sync.dma_start(T.wt[:], T.w[:]).then_inc(S.sw, 16)
    g.sync.dma_start(T.xt[:, 0:512 * XA], T.x[:, 0:512 * XA]).then_inc(S.sxa, 16)
    g.sync.wait_ge(S.v, tok[i_v0])
    g.sync.dma_start(T.xt[:, 512 * XA:], T.x[:, 512 * XA:]).then_inc(S.sxb, 16)

    waited = {}

    def wait(q, sem, n):
        if waited.get((q, sem), 0) < n:
            (vec if q == "v" else sca).wait_ge(S[sem], n)
            waited[q, sem] = n

    for i in order:
        q, call, args, kw, reads, writes, ex, cost, tail, lag = ops[i]
        for sem, n in ex:
            wait(q, sem, n)
        for s in ("v", "a"):
            wait(q, s, max([0] + [tok[j] for j in raw[i] if queue[j] == s]))
        call(*args, **kw).then_inc(S[q], 1)

    big = {"allow_small_or_imprecise_dtypes": True}
    g.iota(T.pi[:, 0:1], [[0, 1]], 0, 1).then_inc(S.gi, 1)
    g.iota(T.mod32[:], [[0, 2], [1, 32]], 0, 0, **big).then_inc(S.gi, 1)
    g.iota(T.mod8[:], [[0, 12], [1, 8]], 0, 0, **big).then_inc(S.gi, 1)
    g.iota(T.n96[:], [[0, 2], [1, 6], [0, 8]], 1, 0, **big).then_inc(S.gi, 1)
    g.iota(T.mod16[:], [[16, 16]], 0, 0, **big).then_inc(S.gi, 1)
    left = [0]
    others = sorted([q for q in range(NR) if q != r], key=lambda q: (q // 2 != 1, (q - r) % NR))
    mycol = T.lst[:, LC * r:LC * r + LC]
    g.wait_ge(S.sdm, 128)
    g.remote_dma_fused([RemoteDMATransfer(
        dst_ids=[DstId(rid=addr(q)[0], pnc=addr(q)[1]) for q in others], dma_engine_mask=topo.mask(core, cores[others[0]]),
        remote_sem=S.al, srcs=[mycol], dsts=[mycol] * len(others))], local_sem=S.loc)
    left[0] += n_off
    g.wait_ge(S.v, tok[i_w])
    mys = slice(*my)
    rid, pid = addr(mate)
    mk = topo.mask(core, cores[mate])
    g.remote_dma(T.p1c[:, mys].bitcast(dt.uint8), T.p1c[:, mys].bitcast(dt.uint8), S.aw, S.loc, pid, rid, mk)
    g.remote_dma(T.p1s[:, mys], T.p1s[:, mys], S.aw, S.loc, pid, rid, mk)
    left[0] += 2 * n_off

    def send(i, jobs):
        key = "snd%d" % i
        g.wait_ge(S.v, tok[picks[key][0]])
        eng = topo.engines(core, cores[jobs[0][1]])
        per = len(eng) // len(jobs)
        for kind in ("c", "s"):
            if kind == "s":
                g.wait_ge(S.a, tok[picks[key][1]])
            trs = []
            for n, (a, q, p) in enumerate(jobs):
                src, dst = T[key + kind][:, a:a + BLK], T["p2" + kind][:, p:p + BLK]
                if kind == "c":
                    src, dst = src.bitcast(dt.uint8), dst.bitcast(dt.uint8)
                trs.append(RemoteDMATransfer(dst_ids=[DstId(rid=addr(q)[0], pnc=addr(q)[1])], srcs=[src], dsts=[dst],
                                             dma_engine_mask=sum(1 << x for x in eng[per * n:per * n + per]), remote_sem=S["ar%d" % i]))
            g.remote_dma_fused(trs, local_sem=S.loc)
            left[0] += per * len(jobs)

    GA = 6 * PC
    jobs = []
    for n, b in enumerate(near_blocks):
        for q in peers(pair - 1 if b == pair - 1 else pair + 1):
            jobs.append((GA * n, q, OWN + BLK * b))
    send(1, jobs)
    jobs = []
    for b in range(2):
        if mid:
            dst, col = 2 * b, W1
        elif b == near:
            dst, col = 1, W1 + (BLK if pair == 2 else 0)
        else:
            dst, col = 2 - pair, W1 + BLK
        for q in peers(dst):
            jobs.append((GA * b, q, col))
    send(3, jobs)

    for t in range(RD):
        g.tensor.wait_ge(S.v, max(tok[picks[t][0]], tok[i_xa if t < XA else i_xb]))
        g.tensor.wait_ge(S.a, tok[picks[t][1]])
        for h in range(2):
            if t == 4:
                g.tensor.wait_ge(S.a, tok[evac[0, h]])
            st, c = slice(128 * h, 128 * h + 128), slice(128 * t, 128 * t + 128)
            g.tensor.matmul_mx(out_of(t, h)[1], T["st%dc" % t][:, st], T["st%ds" % t][:, st], T.xqc[:, c], T.xqs[:, c], True, True).then_inc(S.mm, 1)

    for t in range(RD):
        for h in range(2):
            i = evac[t, h]
            g.sync.wait_ge(S[queue[i]], tok[i])
        g.sync.dma_start(T.y[:, 256 * t:256 * t + 256], T.yb[:, 256 * t:256 * t + 256]).then_inc(S.sy, 16)
    g.sync.wait_ge(S.v, count["v"])
    g.sync.wait_ge(S.a, count["a"])
    g.sync.wait_ge(S.sy, 16 * RD)
    g.wait_ge(S.loc, left[0])
